import numpy as np
import ml_dtypes


def mxq(x, axis, fmt="e4m3"):
    dtype, down = {"e4m3": (ml_dtypes.float8_e4m3fn, 7), "e5m2": (ml_dtypes.float8_e5m2, 14)}[fmt]
    v = np.moveaxis(np.asarray(x, np.float32).astype(ml_dtypes.bfloat16).astype(np.float64), axis, -1)
    blocks = v.reshape(v.shape[:-1] + (-1, 32))
    amax = np.abs(blocks).max(-1, keepdims=True)
    byte = np.maximum(np.where(amax > 0, np.frexp(amax)[1] - 1 + 127, 0) - down, 1)
    scale = np.exp2(byte - 127.0)
    codes = (blocks / scale).astype(np.float32).astype(dtype).astype(np.float64)
    return np.moveaxis((codes * scale).reshape(v.shape), -1, axis)


WIDE = False


def mx_kscale(k):
    if not WIDE:
        return np.ones(k)
    levels = np.array([10, -10, 5, -5, 0])
    if k % 512:
        return np.exp2(np.random.permutation(np.resize(levels, k // 32))).repeat(32)
    a = np.empty((k // 512, 16))
    for p in range(k // 512):
        a[p, :8] = np.random.permutation(np.resize(levels, 8))
        for g in range(8):
            far = levels[np.abs(levels - a[p, g]) >= 10]
            a[p, g + 8] = far[np.random.randint(len(far))]
    return np.exp2(a.ravel()).repeat(32)


BF16 = ml_dtypes.bfloat16


def bf(x):
    return np.asarray(x, np.float32).astype(BF16)


def f64(x):
    return np.asarray(x).astype(np.float64)


E2M1 = np.array([0.0, 0.5, 1.0, 1.5, 2.0, 3.0, 4.0, 6.0, -0.0, -0.5, -1.0, -1.5, -2.0, -3.0, -4.0, -6.0])


def pack_weight(w, fmt):
    k, n = w.shape
    w = f64(bf(w)).reshape(k // 32, 32, n)
    amax = np.abs(w).max(1)
    if fmt == "e4m3":
        byte = np.frexp(amax)[1] - 1 + 127 - 7
    else:
        mant, ex = np.frexp(amax / 6.0)
        byte = np.where(mant > 0.5, ex, ex - 1) + 127
    byte = np.clip(np.where(amax > 0, byte, 1), 1, 254)
    scaled = (w * np.exp2(127.0 - byte)[:, None, :]).reshape(k, n).astype(np.float32)
    by_word = np.ascontiguousarray(scaled.reshape(k // 512, 128, 4, n).transpose(0, 1, 3, 2))
    if fmt == "e4m3":
        words = by_word.astype(ml_dtypes.float8_e4m3fn).view(np.uint8)
    else:
        c = by_word.astype(ml_dtypes.float4_e2m1fn).view(np.uint8) & 0xF
        words = c[..., 0::2] | (c[..., 1::2] << 4)
    return np.ascontiguousarray(words), np.ascontiguousarray(byte.astype(np.uint8).reshape(k // 512, 16, n))


def unpack_weight(words, scales, fmt):
    g, p, n, _ = words.shape
    if fmt == "e4m3":
        vals = np.ascontiguousarray(words).view(ml_dtypes.float8_e4m3fn).astype(np.float64)
    else:
        nib = np.empty((g, p, n, 4), np.uint8)
        nib[..., 0::2] = words & 0xF
        nib[..., 1::2] = words >> 4
        vals = E2M1[nib]
    vals = vals * np.repeat(np.exp2(scales.astype(np.float64) - 127.0), 8, axis=1)[..., None]
    return vals.transpose(0, 1, 3, 2).reshape(g * 512, n)
def pack4(w):
    words, scales = pack_weight(w, "e2m1")
    return words.reshape(words.shape[0], 128, -1), scales


def unpack4(words, scales):
    return unpack_weight(words.reshape(words.shape[0], 128, -1, 2), scales, "e2m1")


E4M3FN = np.array([(-1.0 if i & 128 else 1.0) * ((1.0 + (i & 7) / 8.0) * 2.0 ** (((i >> 3) & 15) - 7) if i & 120 else (i & 7) * 2.0 ** -9) for i in range(256)])


def e4m3fn_bytes(y):
    return np.clip(np.asarray(y, np.float64), -448.0, 448.0).astype(np.float32).astype(ml_dtypes.float8_e4m3fn).view(np.uint8)


def e4m3fn_values(b):
    return E4M3FN[b]


N, D, F, T, U, C = 1024, 1024, 1024, 9, 256, 2
TU = T * U
FLOW_SCALE = 16.0
LOGIT_SCALE = 0.25


def draw0():
    s, t = mx_kscale(D), mx_kscale(F)
    x = bf(np.random.standard_normal((N, D)) * s)
    w1_words, w1_scales = pack4(np.random.standard_normal((D, F)) / np.sqrt(D) / s[:, None] * t)
    b1 = bf(0.3 * np.random.standard_normal(F) * t)
    w2_words, w2_scales = pack4(np.random.standard_normal((F, TU)) * 5.0 / np.sqrt(F) / t[:, None])
    return {
        "x": x,
        "w1_words": w1_words,
        "w1_scales": w1_scales,
        "b1": b1,
        "w2_words": w2_words,
        "w2_scales": w2_scales,
        "b2": bf(0.5 * np.random.standard_normal(TU)),
        "nb": bf(np.random.standard_normal((N, T, C)) * 0.15),
    }


def tap_logits(x, w1_words, w1_scales, b1, w2_words, w2_scales, b2):
    h = np.maximum((mxq(f64(x), 1, "e4m3") @ unpack4(w1_words, w1_scales)) + f64(b1), 0.0)
    return LOGIT_SCALE * ((mxq(h, 1, "e4m3") @ unpack4(w2_words, w2_scales)) + f64(b2))


def core(x, w1_words, w1_scales, b1, w2_words, w2_scales, b2, nb):
    l = tap_logits(x, w1_words, w1_scales, b1, w2_words, w2_scales, b2)
    l = np.reshape(l, (N, T, U))
    e = np.exp(l - l.max(axis=1, keepdims=True))
    p = e / e.sum(axis=1, keepdims=True)
    flow = FLOW_SCALE * f64(nb)
    return np.sum(p[..., None] * flow[:, :, None, :], axis=1)


def setup_inputs():
    drawn = draw0()
    full = np.asarray(drawn['x']).astype(np.float64)
    scale = (np.abs(full).reshape(1024, 8, 128).max(axis=(2,)) / 448.0).astype(np.float32)
    given = {}
    for key, value in drawn.items():
        if key == 'x':
            given['x_bytes'] = e4m3fn_bytes(full / np.repeat(scale.astype(np.float64), 128, axis=1))
            given['x_scale'] = scale
        else:
            given[key] = value
    return given


def reference(x_bytes, x_scale, w1_words, w1_scales, b1, w2_words, w2_scales, b2, nb):
    return core(e4m3fn_values(x_bytes) * np.repeat(x_scale.astype(np.float64), 128, axis=1), w1_words, w1_scales, b1, w2_words, w2_scales, b2, nb)

@@ -1,0 +1,769 @@
+from contextlib import ExitStack
+
+import concourse.mybir as mybir
+from concourse.masks import make_identity
+
+N, D, F, T, U, C = 1024, 1024, 1024, 9, 256, 2
+TU = T * U
+FLOPS = 2 * N * D * F + 2 * N * F * TU
+
+F32 = mybir.dt.float32
+BF16 = mybir.dt.bfloat16
+U32 = mybir.dt.uint32
+I32 = mybir.dt.int32
+U8 = mybir.dt.uint8
+FP8 = mybir.dt.float8_e4m3fn
+FP8X4 = mybir.dt.float8_e4m3fn_x4
+FP4X4 = mybir.dt.float4_e2m1fn_x4
+ALU = mybir.AluOpType
+ACT = mybir.ActivationFunctionType
+
+P = 128
+W = 512
+GROUPS = [2, 2, 2, 1, 1]
+GROUP_OF = [0, 0, 1, 1, 2, 2, 3, 4]
+PLACE_OF = [0, 1, 0, 1, 0, 1, 0, 0]
+HIDDEN_ON_VECTOR = {(0, 6), (0, 0), (0, 1), (0, 7), (1, 6), (1, 4), (1, 7)}
+LOGITS_ON_VECTOR = {(0, 7)}
+SUMS_ON_TENSOR = {(4, 1), (5, 1), (6, 1), (7, 1)}
+WIDEN_ON_VECTOR = {0: 4, 6: 4, 5: 4, 7: 4, 4: 4}
+FIRST_ON_VECTOR = {7}
+TURN_ON_VECTOR = {4}
+SIDE_ON_VECTOR = {(7, 2)}
+NTILES = N // P
+
+
+def tile_convextapupsampleflowhead_d1p_kernel(
+    tc, x_bytes, x_scale, w1_words, w1_scales, b1, w2_words, w2_scales, b2, nb, out
+):
+    nc = tc.nc
+    x_view = x_bytes.rearrange("(p i) k -> p i k", i=NTILES)
+    out_view = out.rearrange("(p i) u c -> p i (u c)", i=NTILES)
+
+    with ExitStack() as ctx:
+        keep = ctx.enter_context(tc.tile_pool(name="keep", bufs=1))
+        work = ctx.enter_context(tc.tile_pool(name="work", bufs=2))
+        psum = ctx.enter_context(tc.psum_pool(name="psum", bufs=1))
+
+        w1s = keep.tile([P, 2, F], U8, name="w1s", align_bytes=64)
+        w2s = keep.tile([P, 2, TU], U8, name="w2s", align_bytes=64)
+        nc.vector.memset(w1s[:].bitcast(I32), 0)
+        nc.gpsimd.memset(w2s[:].bitcast(I32), 0)
+        b2rows = keep.tile([P, P], BF16, name="b2rows")
+        nc.gpsimd.memset(b2rows[:], 0.0)
+
+        xsc = keep.tile([P, NTILES, 8], F32, name="xsc")
+        nc.scalar.dma_start(out=xsc[:], in_=x_scale.rearrange("(p i) j -> p i j", i=NTILES))
+        w1t = keep.tile([P, 2, 2 * F], U8, name="w1t", align_bytes=64)
+        xb = []
+        for i in range(NTILES):
+            xbt = keep.tile([P, D], U8, name="xbytes%d" % i, align_bytes=64)
+            xb.append(xbt)
+        w1_view = w1_words.rearrange("g p n -> p g n")
+
+        def load_x(i):
+            nc.sync.dma_start(out=xb[i][:], in_=x_view[:, i, :])
+
+        def load_w1(q):
+            half = slice(D * q, D * (q + 1))
+            nc.sync.dma_start(out=w1t[:, :, half].bitcast(I32), in_=w1_view[:, :, half].bitcast(I32))
+
+        load_x(0)
+        load_w1(0)
+        load_x(1)
+        for q in range(4):
+            nc.sync.dma_start(
+                out=w1s[32 * q : 32 * q + 4, :, :].bitcast(I32),
+                in_=w1_scales[:, 4 * q : 4 * q + 4, :].rearrange("g q n -> q g n").bitcast(I32),
+            )
+        load_x(2)
+        load_x(3)
+        load_w1(1)
+        b1t = keep.tile([P, 2, 4], BF16, name="b1t")
+        nc.scalar.dma_start(out=b1t[:], in_=b1.rearrange("(g p t) -> p g t", p=P, t=4))
+        nc.scalar.dma_start(out=b2rows[0 : 2 * T, :], in_=b2.rearrange("(r u) -> r u", u=P))
+        nbt = keep.tile([P, NTILES, 2 * T], BF16, name="nbt")
+        nc.scalar.dma_start(out=nbt[:], in_=nb.rearrange("(p i) t c -> p i (t c)", i=NTILES))
+        w2t = keep.tile([P, 2, 2 * TU], U8, name="w2t", align_bytes=64)
+        for q in range(4):
+            nc.sync.dma_start(
+                out=w2s[32 * q : 32 * q + 4, :, :].bitcast(I32),
+                in_=w2_scales[:, 4 * q : 4 * q + 4, :].rearrange("g q n -> q g n").bitcast(I32),
+            )
+        for g in range(2):
+            nc.sync.dma_start(out=w2t[:, g, :].bitcast(I32), in_=w2_words[g].bitcast(I32))
+        for i in range(4, NTILES):
+            load_x(i)
+
+        ident = keep.tile([P, P], F32, name="ident")
+        make_identity(nc, ident[:])
+
+
+        w1p = keep.tile([P, 2, 2, 4, 2 * P], U8, name="w1p", align_bytes=64)
+        w1sp = keep.tile([P, 2, 2, 4, P], U8, name="w1sp", align_bytes=64)
+        b2f = keep.tile([P, P], F32, name="b2f")
+        b2t = keep.tile([P, 2 * T], F32, name="b2t")
+        flow = keep.tile([P, NTILES, 2 * T], F32, name="flow")
+
+        def permute(q):
+            for g in range(2):
+                nc.vector.tensor_copy(
+                    out=w1p[:, g, q, :, :].rearrange("p t (m b) -> p t m b", b=2),
+                    in_=w1t[:, g, 1024 * q : 1024 * (q + 1)].rearrange("p (m t b) -> p t m b", t=4, b=2),
+                )
+            nc.vector.tensor_copy(
+                out=w1sp[:, :, q, :, :],
+                in_=w1s[:, :, 512 * q : 512 * (q + 1)].rearrange("p g (m t) -> p g t m", t=4),
+            )
+
+        def biases():
+            nc.gpsimd.tensor_copy(out=b2f[:], in_=b2rows[:])
+            nc.gpsimd.tensor_scalar(out=flow[:], in0=nbt[:], scalar1=16.0, scalar2=0.0, op0=ALU.mult, op1=ALU.add)
+            b2ps = psum.tile([P, 512], F32, name="b2ps", tag="rd", bufs=1)
+            nc.tensor.transpose(b2ps[:, 0:P], b2f[:], ident[:])
+            nc.scalar.copy(out=b2t[:], in_=b2ps[:, 0 : 2 * T])
+
+
+        state = {}
+
+        def widen(i):
+            xw = work.tile([P, D], BF16, name="xw%d" % i, tag="xw", bufs=3, align_bytes=64)
+            for k in range(8):
+                block = slice(P * k, P * (k + 1))
+                if k < WIDEN_ON_VECTOR.get(i, 0):
+                    nc.vector.tensor_scalar(
+                        out=xw[:, block],
+                        in0=xb[i][:, block].bitcast(FP8),
+                        scalar1=xsc[:, i, k : k + 1],
+                        scalar2=None,
+                        op0=ALU.mult,
+                    )
+                else:
+                    nc.scalar.activation(
+                        out=xw[:, block], in_=xb[i][:, block].bitcast(FP8), func=ACT.Copy, scale=xsc[:, i, k : k + 1]
+                    )
+            state["xw", i] = xw
+
+        def turn(i):
+            words = state["xw", i][:].bitcast(F32)
+            xt = psum.tile([P, 2, 2, P], F32, name="xt%d" % i, tag="mm", bufs=3)
+            for g in range(2):
+                for u in range(2):
+                    nc.tensor.transpose(xt[:, g, u, :], words[:, 256 * g + u : 256 * (g + 1) : 2], ident[:])
+            c, j = i // 4, i % 4
+            if ("xg", c) not in state:
+                state["xg", c] = work.tile([P, 2, W, 4], BF16, name="xg%d" % c, tag="xg", bufs=1, align_bytes=64)
+            dst = state["xg", c][:, :, P * j : P * (j + 1), :].rearrange("p g r e -> p g (r e)").bitcast(F32)
+            dst = dst.rearrange("p g (r u) -> p g r u", u=2)
+            src = xt[:].rearrange("p g u r -> p g r u")
+            if i in TURN_ON_VECTOR:
+                nc.vector.tensor_copy(out=dst, in_=src)
+            else:
+                nc.scalar.copy(out=dst, in_=src)
+
+        def quant_x(c, g):
+            if ("xq", c) not in state:
+                state["xq", c] = work.tile([P, 2, W], U32, name="xq%d" % c, tag="xq", bufs=1, align_bytes=64)
+                state["xs", c] = work.tile([P, 2, W], U8, name="xs%d" % c, tag="xs", bufs=1, align_bytes=64)
+            nc.vector.quantize_mx(
+                out=state["xq", c][:, g, :].bitcast(FP8X4),
+                scales=state["xs", c][:, g, :],
+                in_=state["xg", c][:, g, :, :].rearrange("p n t -> p (n t)"),
+            )
+
+        def hidden(c, k):
+            q, t = k // 4, k % 4
+            xq, xs = state["xq", c], state["xs", c]
+            if ("hr", c, q) not in state:
+                state["hr", c, q] = work.tile([P, 4, W], BF16, name="hr%d%d" % (c, q), tag="hr", bufs=2, align_bytes=64)
+            bank = psum.tile([P, W], F32, name="h%d_%d" % (c, k), tag="mm", bufs=3)
+            for g in range(2):
+                nc.tensor.matmul_mx(
+                    out=bank[:],
+                    lhsT=w1p[:, g, q, t, :].bitcast(FP4X4),
+                    lhsT_scale=w1sp[:, g, q, t, :],
+                    rhs=xq[:, g, :].bitcast(FP8X4),
+                    rhs_scale=xs[:, g, :],
+                    start=(g == 0),
+                    stop=(g == 1),
+                )
+            if (c, k) in HIDDEN_ON_VECTOR:
+                nc.vector.tensor_scalar(
+                    out=state["hr", c, q][:, t, :], in0=bank[:], scalar1=b1t[:, q, t : t + 1], scalar2=0.0, op0=ALU.add, op1=ALU.max
+                )
+            else:
+                nc.scalar.activation(out=state["hr", c, q][:, t, :], in_=bank[:], func=ACT.Relu, bias=b1t[:, q, t : t + 1])
+
+        def gather_h(c, k):
+            q, part = k // 2, k % 2
+            if ("hg", c, q) not in state:
+                state["hg", c, q] = work.tile([P, W, 4], BF16, name="hg%d%d" % (c, q), tag="hg", bufs=2, align_bytes=64)
+            cols = slice(256 * part, 256 * (part + 1))
+            nc.vector.tensor_copy(
+                out=state["hg", c, q][:, cols, :], in_=state["hr", c, q][:, :, cols].rearrange("p t n -> p n t")
+            )
+
+        def quant_h(c, q):
+            if ("hq", c) not in state:
+                state["hq", c] = work.tile([P, 2, W], U32, name="hq%d" % c, tag="hq", bufs=2, align_bytes=64)
+                state["hs", c] = work.tile([P, 2, W], U8, name="hs%d" % c, tag="hs", bufs=2, align_bytes=64)
+            nc.vector.quantize_mx(
+                out=state["hq", c][:, q, :].bitcast(FP8X4),
+                scales=state["hs", c][:, q, :],
+                in_=state["hg", c, q][:].rearrange("p n t -> p (n t)"),
+            )
+
+        def logits(c, k):
+            h, t = k // T, k % T
+            hq, hs = state["hq", c], state["hs", c]
+            if ("a", c, h) not in state:
+                state["a", c, h] = work.tile([P, T, W], F32, name="a%d%d" % (c, h), tag="a%d" % h, bufs=2)
+            col = U * t + P * h
+            bank = psum.tile([P, W], F32, name="l%d_%d" % (c, k), tag="mm", bufs=3)
+            for g in range(2):
+                nc.tensor.matmul_mx(
+                    out=bank[:],
+                    lhsT=w2t[:, g, 2 * col : 2 * (col + P)].bitcast(FP4X4),
+                    lhsT_scale=w2s[:, g, col : col + P],
+                    rhs=hq[:, g, :].bitcast(FP8X4),
+                    rhs_scale=hs[:, g, :],
+                    start=(g == 0),
+                    stop=(g == 1),
+                )
+            bias = b2t[:, 2 * t + h : 2 * t + h + 1]
+            if (c, k) in LOGITS_ON_VECTOR:
+                nc.vector.tensor_scalar(out=state["a", c, h][:, t, :], in0=bank[:], scalar1=bias, scalar2=None, op0=ALU.add)
+            else:
+                nc.scalar.activation(out=state["a", c, h][:, t, :], in_=bank[:], func=ACT.Identity, bias=bias)
+
+        def maximum(c, k):
+            h, step = k // 6, k % 6
+            a = state["a", c, h]
+            if step == 0:
+                state["m", c, h] = work.tile([P, 2, W], F32, name="m%d%d" % (c, h), tag="w", bufs=1)
+                if ("nm", c) not in state:
+                    state["nm", c] = work.tile([P, 2, W], F32, name="nm%d" % c, tag="nm", bufs=2)
+            m = state["m", c, h]
+            if step == 0:
+                nc.vector.tensor_tensor(out=m[:], in0=a[:, 0:2, :], in1=a[:, 2:4, :], op=ALU.max)
+            elif step < 3:
+                nc.vector.tensor_tensor(out=m[:], in0=m[:], in1=a[:, 2 * step + 2 : 2 * step + 4, :], op=ALU.max)
+            elif step == 3:
+                nc.vector.tensor_tensor(out=m[:, 0, :], in0=m[:, 0, :], in1=m[:, 1, :], op=ALU.max)
+            elif step == 4:
+                nc.vector.tensor_tensor(out=m[:, 0, :], in0=m[:, 0, :], in1=a[:, 8, :], op=ALU.max)
+            else:
+                nc.vector.tensor_scalar(
+                    out=state["nm", c][:, h, :], in0=m[:, 0, :], scalar1=-1.0, scalar2=None, op0=ALU.mult
+                )
+
+        def weights(i, b):
+            c, j = i // 4, i % 4
+            nm = state["nm", c]
+            cols = slice(P * j, P * (j + 1))
+            if ("e", i) not in state:
+                state["e", i] = work.tile([P, T, U], F32, name="e%d" % i, tag="e", bufs=3)
+                state["acc", i] = work.tile([P, C, U], F32, name="acc%d" % i, tag="acc", bufs=5)
+            e = state["e", i]
+            taps = range(2 * b, min(T, 2 * b + 2))
+            d = psum.tile([P, 2, U], F32, name="d%d_%d" % (i, b), tag="d", bufs=3)
+            for t in taps:
+                for h in range(2):
+                    dst = d[:, t - 2 * b, h * P : (h + 1) * P]
+                    nc.tensor.matmul(dst, state["a", c, h][:, t, cols], ident[:], start=True, stop=False, is_transpose=True)
+                    nc.tensor.matmul(dst, nm[:, h, cols], ident[:], start=False, stop=True, is_transpose=True)
+            k = len(taps)
+            nc.scalar.activation(out=e[:, 2 * b : 2 * b + k, :], in_=d[:, 0:k, :], func=ACT.Exp, scale=0.25)
+
+        def first_product(i):
+            for c in range(C):
+                if (i, c) in SUMS_ON_TENSOR:
+                    continue
+                if i in FIRST_ON_VECTOR:
+                    nc.vector.tensor_scalar(
+                        out=state["acc", i][:, c, :], in0=state["e", i][:, 0, :], scalar1=flow[:, i, c : c + 1], scalar2=None, op0=ALU.mult
+                    )
+                else:
+                    nc.scalar.activation(
+                        out=state["acc", i][:, c, :], in_=state["e", i][:, 0, :], func=ACT.Copy, scale=flow[:, i, c : c + 1]
+                    )
+
+        def products(i, t):
+            e, acc = state["e", i], state["acc", i]
+            for c in range(C):
+                if (i, c) not in SUMS_ON_TENSOR:
+                    nc.vector.scalar_tensor_tensor(
+                        out=acc[:, c, :],
+                        in0=e[:, t, :],
+                        scalar=flow[:, i, C * t + c : C * t + c + 1],
+                        in1=acc[:, c, :],
+                        op0=ALU.mult,
+                        op1=ALU.add,
+                    )
+
+        def side_products(i, b):
+            e = state["e", i]
+            for c in range(C):
+                if (i, c) in SUMS_ON_TENSOR:
+                    if ("w", i, c) not in state:
+                        state["w", i, c] = work.tile([P, T, U], F32, name="w%d%d" % (i, c), tag="w", bufs=1)
+                    for t in range(2 * b, min(T, 2 * b + 2)):
+                        factor = flow[:, i, C * t + c : C * t + c + 1]
+                        dst = state["w", i, c][:, t, :]
+                        if (i, b) in SIDE_ON_VECTOR:
+                            nc.vector.tensor_scalar(out=dst, in0=e[:, t, :], scalar1=factor, scalar2=None, op0=ALU.mult)
+                        else:
+                            nc.scalar.activation(out=dst, in_=e[:, t, :], func=ACT.Copy, scale=factor)
+
+        def side_sums(i):
+            for c in range(C):
+                if (i, c) in SUMS_ON_TENSOR:
+                    bank = psum.tile([P, 512], F32, name="sum%d%d" % (i, c), tag="den", bufs=1)
+                    for h in range(2):
+                        for t in range(T):
+                            nc.tensor.matmul(
+                                bank[:, h * P : (h + 1) * P],
+                                state["w", i, c][:, t, h * P : (h + 1) * P],
+                                ident[:],
+                                start=(t == 0),
+                                stop=(t == T - 1),
+                                is_transpose=True,
+                            )
+                    sums = work.tile([P, 2, P], F32, name="sums%d%d" % (i, c), tag="sums", bufs=4)
+                    nc.scalar.copy(out=sums[:].rearrange("p h n -> p (h n)"), in_=bank[:, 0:U])
+                    state["sums", i, c] = sums
+
+        def side_turn(i):
+            for c in range(C):
+                if (i, c) in SUMS_ON_TENSOR:
+                    bank = psum.tile([P, 512], F32, name="back%d%d" % (i, c), tag="rd", bufs=1)
+                    for h in range(2):
+                        nc.tensor.transpose(bank[:, h * P : (h + 1) * P], state["sums", i, c][:, h, :], ident[:])
+                    nc.scalar.copy(out=state["acc", i][:, c, :], in_=bank[:, 0:U])
+
+        def denominator(i):
+            e = state["e", i]
+            n = GROUP_OF[i]
+            if ("ds", n) not in state:
+                state["ds", n] = work.tile([P, U * GROUPS[n]], F32, name="ds%d" % n, tag="ds", bufs=2)
+            den = psum.tile([P, 2, P], F32, name="den%d" % i, tag="den", bufs=1)
+            for h in range(2):
+                for t in range(T):
+                    nc.tensor.matmul(
+                        den[:, h, :], e[:, t, h * P : (h + 1) * P], ident[:], start=(t == 0), stop=(t == T - 1), is_transpose=True
+                    )
+            at = U * PLACE_OF[i]
+            nc.scalar.copy(out=state["ds", n][:, at : at + U], in_=den[:].rearrange("p h n -> p (h n)"))
+
+        def inverse(i, k):
+            n = GROUP_OF[i]
+            levels = 2 if GROUPS[n] == 1 else 3
+            if PLACE_OF[i] != GROUPS[n] - 1 or k > 2 * levels:
+                return
+            if k == 0:
+                state["tree", n] = [state["ds", n]]
+            tree = state["tree", n]
+            if k < levels:
+                src = tree[k]
+                half = src.shape[1] // 2
+                dst = work.tile([P, half], F32, name="tree%d_%d" % (n, k), tag="tree%d" % half, bufs=2)
+                nc.vector.tensor_tensor(out=dst[:], in0=src[:, 0:half], in1=src[:, half : 2 * half], op=ALU.mult)
+                tree.append(dst)
+            elif k == levels:
+                dst = work.tile([P, 64], F32, name="inv%d" % n, tag="inv", bufs=3)
+                nc.vector.reciprocal(out=dst[:], in_=tree[levels][:])
+                state["inv", n] = dst
+            else:
+                src = tree[2 * levels - k]
+                half = src.shape[1] // 2
+                dst = work.tile([P, 2 * half], F32, name="inv%d_%d" % (n, k), tag="inv%d" % half, bufs=2)
+                nc.vector.tensor_tensor(
+                    out=dst[:].rearrange("p (a b) -> p a b", a=2),
+                    in0=src[:].rearrange("p (a b) -> p a b", a=2)[:, ::-1, :],
+                    in1=state["inv", n][:].unsqueeze(1).to_broadcast([P, 2, half]),
+                    op=ALU.mult,
+                )
+                state["inv", n] = dst
+
+        def turn_inverse(i):
+            n = GROUP_OF[i]
+            rd = psum.tile([P, 512], F32, name="rd%d" % i, tag="rd", bufs=1)
+            for h in range(2):
+                at = U * PLACE_OF[i] + P * h
+                nc.tensor.transpose(rd[:, h * P : (h + 1) * P], state["inv", n][:, at : at + P], ident[:])
+            state["rd", i] = rd
+
+        def finish(i):
+            o = work.tile([P, U, C], F32, name="o%d" % i, tag="o", bufs=2)
+            nc.vector.tensor_tensor(
+                out=o[:],
+                in0=state["acc", i][:].rearrange("p c u -> p u c"),
+                in1=state["rd", i][:, 0:U].unsqueeze(2).to_broadcast([P, U, C]),
+                op=ALU.mult,
+            )
+            nc.sync.dma_start(out=out_view[:, i, :], in_=o[:].rearrange("p u c -> p (u c)"))
+
+        def go(i, step, *args):
+            if 0 <= i < NTILES:
+                step(i, *args)
+
+        with tc.manual_schedule():
+            widen(0)
+            permute(0)
+            widen(1)
+            turn(0)
+            widen(3)
+            widen(2)
+            turn(3)
+            turn(2)
+            turn(1)
+            permute(1)
+            biases()
+            quant_x(0, 0)
+            quant_x(0, 1)
+            hidden(0, 6)
+            hidden(0, 0)
+            hidden(0, 7)
+            widen(4)
+            widen(7)
+            hidden(0, 5)
+            hidden(0, 1)
+            widen(5)
+            hidden(0, 4)
+            turn(4)
+            widen(6)
+            turn(7)
+            turn(5)
+            turn(6)
+            hidden(0, 2)
+            hidden(0, 3)
+            gather_h(0, 3)
+            gather_h(0, 2)
+            quant_x(1, 0)
+            quant_x(1, 1)
+            quant_h(0, 1)
+            gather_h(0, 1)
+            hidden(1, 3)
+            gather_h(0, 0)
+            hidden(1, 2)
+            quant_h(0, 0)
+            hidden(1, 0)
+            hidden(1, 5)
+            hidden(1, 4)
+            hidden(1, 7)
+            hidden(1, 6)
+            hidden(1, 1)
+            gather_h(1, 2)
+            gather_h(1, 0)
+            gather_h(1, 3)
+            gather_h(1, 1)
+            quant_h(1, 1)
+            quant_h(1, 0)
+            logits(0, 3)
+            logits(0, 1)
+            logits(0, 15)
+            logits(0, 4)
+            logits(0, 0)
+            logits(0, 2)
+            logits(0, 7)
+            logits(0, 5)
+            logits(0, 9)
+            logits(0, 6)
+            logits(0, 10)
+            logits(0, 13)
+            logits(0, 8)
+            logits(0, 12)
+            logits(0, 11)
+            logits(0, 17)
+            logits(0, 14)
+            logits(0, 16)
+            logits(1, 4)
+            logits(1, 3)
+            logits(1, 5)
+            logits(1, 6)
+            logits(1, 1)
+            logits(1, 0)
+            logits(1, 2)
+            logits(1, 11)
+            logits(1, 15)
+            maximum(0, 0)
+            logits(1, 7)
+            logits(1, 12)
+            logits(1, 10)
+            logits(1, 14)
+            maximum(0, 1)
+            maximum(0, 2)
+            logits(1, 8)
+            logits(1, 9)
+            maximum(0, 3)
+            maximum(0, 4)
+            maximum(0, 5)
+            logits(1, 16)
+            maximum(0, 6)
+            maximum(0, 7)
+            maximum(0, 8)
+            maximum(0, 9)
+            maximum(0, 10)
+            maximum(0, 11)
+            logits(1, 13)
+            logits(1, 17)
+            maximum(1, 0)
+            maximum(1, 1)
+            maximum(1, 2)
+            maximum(1, 3)
+            maximum(1, 4)
+            weights(0, 2)
+            maximum(1, 5)
+            maximum(1, 6)
+            weights(0, 0)
+            maximum(1, 7)
+            weights(0, 1)
+            first_product(0)
+            weights(0, 3)
+            weights(0, 4)
+            side_products(0, 1)
+            maximum(1, 8)
+            products(0, 3)
+            side_products(0, 2)
+            side_products(0, 0)
+            products(0, 6)
+            weights(1, 2)
+            products(0, 5)
+            denominator(0)
+            side_products(0, 3)
+            maximum(1, 9)
+            weights(1, 0)
+            products(0, 7)
+            side_products(0, 4)
+            inverse(0, 0)
+            weights(1, 1)
+            maximum(1, 10)
+            first_product(1)
+            weights(1, 3)
+            side_sums(0)
+            weights(1, 4)
+            inverse(0, 1)
+            side_products(1, 1)
+            products(0, 1)
+            inverse(0, 2)
+            products(1, 3)
+            side_products(1, 2)
+            products(0, 8)
+            side_products(1, 0)
+            inverse(0, 3)
+            products(1, 6)
+            weights(2, 2)
+            products(0, 2)
+            inverse(0, 4)
+            products(1, 5)
+            denominator(1)
+            inverse(0, 5)
+            side_products(1, 3)
+            weights(2, 0)
+            products(0, 4)
+            products(1, 7)
+            inverse(0, 6)
+            side_products(1, 4)
+            inverse(1, 0)
+            weights(2, 1)
+            first_product(2)
+            maximum(1, 11)
+            weights(2, 3)
+            side_sums(1)
+            weights(2, 4)
+            inverse(1, 1)
+            side_products(2, 1)
+            products(1, 1)
+            inverse(1, 2)
+            products(2, 3)
+            side_products(2, 2)
+            products(1, 8)
+            side_products(2, 0)
+            inverse(1, 3)
+            products(2, 6)
+            weights(3, 2)
+            products(1, 2)
+            inverse(1, 4)
+            products(2, 5)
+            denominator(2)
+            inverse(1, 5)
+            side_products(2, 3)
+            weights(3, 0)
+            products(1, 4)
+            products(2, 7)
+            inverse(1, 6)
+            side_products(2, 4)
+            inverse(2, 0)
+            weights(3, 1)
+            first_product(3)
+            weights(3, 3)
+            side_sums(2)
+            weights(3, 4)
+            inverse(2, 1)
+            side_products(3, 1)
+            products(2, 1)
+            inverse(2, 2)
+            products(3, 3)
+            side_turn(0)
+            side_products(3, 2)
+            products(2, 8)
+            side_products(3, 0)
+            inverse(2, 3)
+            products(3, 6)
+            weights(4, 2)
+            products(2, 2)
+            inverse(2, 4)
+            products(3, 5)
+            denominator(3)
+            inverse(2, 5)
+            side_products(3, 3)
+            weights(4, 0)
+            products(2, 4)
+            products(3, 7)
+            inverse(2, 6)
+            side_products(3, 4)
+            inverse(3, 0)
+            weights(4, 1)
+            turn_inverse(0)
+            finish(0)
+            first_product(4)
+            weights(4, 3)
+            side_sums(3)
+            weights(4, 4)
+            inverse(3, 1)
+            side_products(4, 1)
+            products(3, 1)
+            inverse(3, 2)
+            products(4, 3)
+            side_turn(1)
+            side_products(4, 2)
+            products(3, 8)
+            side_products(4, 0)
+            inverse(3, 3)
+            products(4, 6)
+            weights(5, 2)
+            products(3, 2)
+            inverse(3, 4)
+            products(4, 5)
+            denominator(4)
+            inverse(3, 5)
+            side_products(4, 3)
+            weights(5, 0)
+            products(3, 4)
+            products(4, 7)
+            inverse(3, 6)
+            side_products(4, 4)
+            inverse(4, 0)
+            weights(5, 1)
+            turn_inverse(1)
+            finish(1)
+            first_product(5)
+            weights(5, 3)
+            side_sums(4)
+            weights(5, 4)
+            inverse(4, 1)
+            side_products(5, 1)
+            products(4, 1)
+            inverse(4, 2)
+            products(5, 3)
+            side_turn(2)
+            side_products(5, 2)
+            products(4, 8)
+            side_products(5, 0)
+            inverse(4, 3)
+            products(5, 6)
+            weights(6, 2)
+            products(4, 2)
+            inverse(4, 4)
+            products(5, 5)
+            denominator(5)
+            inverse(4, 5)
+            side_products(5, 3)
+            weights(6, 0)
+            products(4, 4)
+            products(5, 7)
+            inverse(4, 6)
+            side_products(5, 4)
+            inverse(5, 0)
+            weights(6, 1)
+            turn_inverse(2)
+            finish(2)
+            first_product(6)
+            weights(6, 3)
+            side_sums(5)
+            weights(6, 4)
+            inverse(5, 1)
+            side_products(6, 1)
+            products(5, 1)
+            inverse(5, 2)
+            products(6, 3)
+            side_turn(3)
+            side_products(6, 2)
+            products(5, 8)
+            side_products(6, 0)
+            inverse(5, 3)
+            products(6, 6)
+            weights(7, 2)
+            products(5, 2)
+            inverse(5, 4)
+            products(6, 5)
+            denominator(6)
+            inverse(5, 5)
+            side_products(6, 3)
+            weights(7, 0)
+            products(5, 4)
+            products(6, 7)
+            inverse(5, 6)
+            side_products(6, 4)
+            inverse(6, 0)
+            weights(7, 1)
+            turn_inverse(3)
+            finish(3)
+            first_product(7)
+            weights(7, 3)
+            side_sums(6)
+            weights(7, 4)
+            inverse(6, 1)
+            side_products(7, 1)
+            products(6, 1)
+            inverse(6, 2)
+            products(7, 3)
+            side_turn(4)
+            side_products(7, 2)
+            products(6, 8)
+            side_products(7, 0)
+            inverse(6, 3)
+            products(7, 6)
+            products(6, 2)
+            inverse(6, 4)
+            products(7, 5)
+            denominator(7)
+            inverse(6, 5)
+            side_products(7, 3)
+            products(6, 4)
+            products(7, 7)
+            inverse(6, 6)
+            side_products(7, 4)
+            inverse(7, 0)
+            turn_inverse(4)
+            finish(4)
+            side_sums(7)
+            inverse(7, 1)
+            products(7, 1)
+            inverse(7, 2)
+            side_turn(5)
+            products(7, 8)
+            inverse(7, 3)
+            products(7, 2)
+            inverse(7, 4)
+            inverse(7, 5)
+            products(7, 4)
+            inverse(7, 6)
+            turn_inverse(5)
+            finish(5)
+            side_turn(6)
+            turn_inverse(6)
+            finish(6)
+            side_turn(7)
+            turn_inverse(7)
+            finish(7)

@@ -19,17 +19,18 @@ ALU = mybir.AluOpType
 ACT = mybir.ActivationFunctionType
 
 P = 128
-W = 512
 GROUPS = [2, 2, 2, 1, 1]
 GROUP_OF = [0, 0, 1, 1, 2, 2, 3, 4]
 PLACE_OF = [0, 1, 0, 1, 0, 1, 0, 0]
-HIDDEN_ON_VECTOR = {(0, 6), (0, 0), (0, 1), (0, 7), (1, 6), (1, 4), (1, 7)}
-LOGITS_ON_VECTOR = {(0, 7)}
-SUMS_ON_TENSOR = {(4, 1), (5, 1), (6, 1), (7, 1)}
-WIDEN_ON_VECTOR = {0: 4, 6: 4, 5: 4, 7: 4, 4: 4}
-FIRST_ON_VECTOR = {7}
-TURN_ON_VECTOR = {4}
-SIDE_ON_VECTOR = {(7, 2)}
+HIDDEN_ON_VECTOR = {-1}
+LOGITS_ON_VECTOR = {(0, 1), (0, 0), (0, 3), (0, 2), (1, 1), (1, 0), (1, 3), (1, 2)}
+SUMS_ON_TENSOR = {(6, 1), (7, 1)}
+WIDEN_ON_VECTOR = {2: 4, 3: 4, 6: 4, 7: 4}
+FIRST_ON_VECTOR = {0}
+TURN_ON_VECTOR = {2}
+SIDE_ON_VECTOR = {(7, 0)}
+GATHER_ON_SCALAR = {(1, 1), (2, 0), (2, 1), (5, 1), (6, 1), (7, 1)}
+NEGATE_ON_SCALAR = {0, 3, 6}
 NTILES = N // P
 
 
@@ -53,7 +54,7 @@ def tile_convextapupsampleflowhead_d1p_kernel(
         nc.gpsimd.memset(b2rows[:], 0.0)
 
         xsc = keep.tile([P, NTILES, 8], F32, name="xsc")
-        nc.scalar.dma_start(out=xsc[:], in_=x_scale.rearrange("(p i) j -> p i j", i=NTILES))
+        nc.sync.dma_start(out=xsc[:], in_=x_scale.rearrange("(p i) j -> p i j", i=NTILES))
         w1t = keep.tile([P, 2, 2 * F], U8, name="w1t", align_bytes=64)
         xb = []
         for i in range(NTILES):
@@ -70,15 +71,14 @@ def tile_convextapupsampleflowhead_d1p_kernel(
 
         load_x(0)
         load_w1(0)
-        load_x(1)
         for q in range(4):
             nc.sync.dma_start(
                 out=w1s[32 * q : 32 * q + 4, :, :].bitcast(I32),
                 in_=w1_scales[:, 4 * q : 4 * q + 4, :].rearrange("g q n -> q g n").bitcast(I32),
             )
-        load_x(2)
-        load_x(3)
+        load_x(1)
         load_w1(1)
+        load_x(2)
         b1t = keep.tile([P, 2, 4], BF16, name="b1t")
         nc.scalar.dma_start(out=b1t[:], in_=b1.rearrange("(g p t) -> p g t", p=P, t=4))
         nc.scalar.dma_start(out=b2rows[0 : 2 * T, :], in_=b2.rearrange("(r u) -> r u", u=P))
@@ -92,7 +92,7 @@ def tile_convextapupsampleflowhead_d1p_kernel(
             )
         for g in range(2):
             nc.sync.dma_start(out=w2t[:, g, :].bitcast(I32), in_=w2_words[g].bitcast(I32))
-        for i in range(4, NTILES):
+        for i in range(3, NTILES):
             load_x(i)
 
         ident = keep.tile([P, P], F32, name="ident")
@@ -111,7 +111,8 @@ def tile_convextapupsampleflowhead_d1p_kernel(
                     out=w1p[:, g, q, :, :].rearrange("p t (m b) -> p t m b", b=2),
                     in_=w1t[:, g, 1024 * q : 1024 * (q + 1)].rearrange("p (m t b) -> p t m b", t=4, b=2),
                 )
-            nc.vector.tensor_copy(
+            engine = nc.vector if q == 0 else nc.gpsimd
+            engine.tensor_copy(
                 out=w1sp[:, :, q, :, :],
                 in_=w1s[:, :, 512 * q : 512 * (q + 1)].rearrange("p g (m t) -> p g t m", t=4),
             )
@@ -127,7 +128,7 @@ def tile_convextapupsampleflowhead_d1p_kernel(
         state = {}
 
         def widen(i):
-            xw = work.tile([P, D], BF16, name="xw%d" % i, tag="xw", bufs=3, align_bytes=64)
+            xw = work.tile([P, D], BF16, name="xw%d" % i, tag="xw", bufs=4, align_bytes=64)
             for k in range(8):
                 block = slice(P * k, P * (k + 1))
                 if k < WIDEN_ON_VECTOR.get(i, 0):
@@ -150,117 +151,117 @@ def tile_convextapupsampleflowhead_d1p_kernel(
             for g in range(2):
                 for u in range(2):
                     nc.tensor.transpose(xt[:, g, u, :], words[:, 256 * g + u : 256 * (g + 1) : 2], ident[:])
-            c, j = i // 4, i % 4
-            if ("xg", c) not in state:
-                state["xg", c] = work.tile([P, 2, W, 4], BF16, name="xg%d" % c, tag="xg", bufs=1, align_bytes=64)
-            dst = state["xg", c][:, :, P * j : P * (j + 1), :].rearrange("p g r e -> p g (r e)").bitcast(F32)
-            dst = dst.rearrange("p g (r u) -> p g r u", u=2)
+            xg = work.tile([P, 2, P, 4], BF16, name="xg%d" % i, tag="xg", bufs=3, align_bytes=64)
+            dst = xg[:].rearrange("p g r e -> p g (r e)").bitcast(F32).rearrange("p g (r u) -> p g r u", u=2)
             src = xt[:].rearrange("p g u r -> p g r u")
             if i in TURN_ON_VECTOR:
                 nc.vector.tensor_copy(out=dst, in_=src)
             else:
                 nc.scalar.copy(out=dst, in_=src)
+            state["xg", i] = xg
 
-        def quant_x(c, g):
-            if ("xq", c) not in state:
-                state["xq", c] = work.tile([P, 2, W], U32, name="xq%d" % c, tag="xq", bufs=1, align_bytes=64)
-                state["xs", c] = work.tile([P, 2, W], U8, name="xs%d" % c, tag="xs", bufs=1, align_bytes=64)
+        def quant_x(i):
+            xq = work.tile([P, 2 * P], U32, name="xq%d" % i, tag="xq", bufs=3, align_bytes=64)
+            xs = work.tile([P, 2 * P], U8, name="xs%d" % i, tag="xs", bufs=3, align_bytes=64)
             nc.vector.quantize_mx(
-                out=state["xq", c][:, g, :].bitcast(FP8X4),
-                scales=state["xs", c][:, g, :],
-                in_=state["xg", c][:, g, :, :].rearrange("p n t -> p (n t)"),
+                out=xq[:].bitcast(FP8X4), scales=xs[:], in_=state["xg", i][:].rearrange("p g n t -> p (g n t)")
             )
+            hq = work.tile([P, 2 * P], U32, name="hq%d" % i, tag="hq", bufs=5, align_bytes=64)
+            hs = work.tile([P, 2 * P], U8, name="hs%d" % i, tag="hs", bufs=5, align_bytes=64)
+            state["x", i] = (xq, xs)
+            state["h", i] = (hq, hs)
 
-        def hidden(c, k):
-            q, t = k // 4, k % 4
-            xq, xs = state["xq", c], state["xs", c]
-            if ("hr", c, q) not in state:
-                state["hr", c, q] = work.tile([P, 4, W], BF16, name="hr%d%d" % (c, q), tag="hr", bufs=2, align_bytes=64)
-            bank = psum.tile([P, W], F32, name="h%d_%d" % (c, k), tag="mm", bufs=3)
-            for g in range(2):
-                nc.tensor.matmul_mx(
-                    out=bank[:],
-                    lhsT=w1p[:, g, q, t, :].bitcast(FP4X4),
-                    lhsT_scale=w1sp[:, g, q, t, :],
-                    rhs=xq[:, g, :].bitcast(FP8X4),
-                    rhs_scale=xs[:, g, :],
-                    start=(g == 0),
-                    stop=(g == 1),
-                )
-            if (c, k) in HIDDEN_ON_VECTOR:
-                nc.vector.tensor_scalar(
-                    out=state["hr", c, q][:, t, :], in0=bank[:], scalar1=b1t[:, q, t : t + 1], scalar2=0.0, op0=ALU.add, op1=ALU.max
-                )
+        def hidden(i, q):
+            xq, xs = state["x", i]
+            bank = psum.tile([P, 4, P], F32, name="h%d%d" % (i, q), tag="mm", bufs=3)
+            for t in range(4):
+                for g in range(2):
+                    nc.tensor.matmul_mx(
+                        out=bank[:, t, :],
+                        lhsT=w1p[:, g, q, t, :].bitcast(FP4X4),
+                        lhsT_scale=w1sp[:, g, q, t, :],
+                        rhs=xq[:, g * P : (g + 1) * P].bitcast(FP8X4),
+                        rhs_scale=xs[:, g * P : (g + 1) * P],
+                        start=(g == 0),
+                        stop=(g == 1),
+                    )
+            hr = work.tile([P, 4, P], BF16, name="hr%d%d" % (i, q), tag="hr", bufs=4, align_bytes=64)
+            for t in range(4):
+                if (i, q) in HIDDEN_ON_VECTOR:
+                    nc.vector.tensor_scalar(
+                        out=hr[:, t, :], in0=bank[:, t, :], scalar1=b1t[:, q, t : t + 1], scalar2=0.0, op0=ALU.add, op1=ALU.max
+                    )
+                else:
+                    nc.scalar.activation(out=hr[:, t, :], in_=bank[:, t, :], func=ACT.Relu, bias=b1t[:, q, t : t + 1])
+            state["hr", i, q] = hr
+
+        def gather_h(i, q):
+            hg = work.tile([P, P, 4], BF16, name="hg%d%d" % (i, q), tag="hg", bufs=4, align_bytes=64)
+            src = state["hr", i, q][:].rearrange("p t n -> p n t")
+            if (i, q) in GATHER_ON_SCALAR:
+                nc.scalar.copy(out=hg[:], in_=src)
             else:
-                nc.scalar.activation(out=state["hr", c, q][:, t, :], in_=bank[:], func=ACT.Relu, bias=b1t[:, q, t : t + 1])
+                nc.vector.tensor_copy(out=hg[:], in_=src)
+            state["hg", i, q] = hg
 
-        def gather_h(c, k):
-            q, part = k // 2, k % 2
-            if ("hg", c, q) not in state:
-                state["hg", c, q] = work.tile([P, W, 4], BF16, name="hg%d%d" % (c, q), tag="hg", bufs=2, align_bytes=64)
-            cols = slice(256 * part, 256 * (part + 1))
-            nc.vector.tensor_copy(
-                out=state["hg", c, q][:, cols, :], in_=state["hr", c, q][:, :, cols].rearrange("p t n -> p n t")
-            )
-
-        def quant_h(c, q):
-            if ("hq", c) not in state:
-                state["hq", c] = work.tile([P, 2, W], U32, name="hq%d" % c, tag="hq", bufs=2, align_bytes=64)
-                state["hs", c] = work.tile([P, 2, W], U8, name="hs%d" % c, tag="hs", bufs=2, align_bytes=64)
+        def quant_h(i, q):
+            hq, hs = state["h", i]
             nc.vector.quantize_mx(
-                out=state["hq", c][:, q, :].bitcast(FP8X4),
-                scales=state["hs", c][:, q, :],
-                in_=state["hg", c, q][:].rearrange("p n t -> p (n t)"),
+                out=hq[:, q * P : (q + 1) * P].bitcast(FP8X4),
+                scales=hs[:, q * P : (q + 1) * P],
+                in_=state["hg", i, q][:].rearrange("p n t -> p (n t)"),
             )
 
-        def logits(c, k):
-            h, t = k // T, k % T
-            hq, hs = state["hq", c], state["hs", c]
-            if ("a", c, h) not in state:
-                state["a", c, h] = work.tile([P, T, W], F32, name="a%d%d" % (c, h), tag="a%d" % h, bufs=2)
-            col = U * t + P * h
-            bank = psum.tile([P, W], F32, name="l%d_%d" % (c, k), tag="mm", bufs=3)
-            for g in range(2):
-                nc.tensor.matmul_mx(
-                    out=bank[:],
-                    lhsT=w2t[:, g, 2 * col : 2 * (col + P)].bitcast(FP4X4),
-                    lhsT_scale=w2s[:, g, col : col + P],
-                    rhs=hq[:, g, :].bitcast(FP8X4),
-                    rhs_scale=hs[:, g, :],
-                    start=(g == 0),
-                    stop=(g == 1),
-                )
-            bias = b2t[:, 2 * t + h : 2 * t + h + 1]
-            if (c, k) in LOGITS_ON_VECTOR:
-                nc.vector.tensor_scalar(out=state["a", c, h][:, t, :], in0=bank[:], scalar1=bias, scalar2=None, op0=ALU.add)
-            else:
-                nc.scalar.activation(out=state["a", c, h][:, t, :], in_=bank[:], func=ACT.Identity, bias=bias)
+        def logits(i, b):
+            hq, hs = state["h", i]
+            if ("a", i) not in state:
+                state["a", i] = work.tile([P, 2 * T, P], F32, name="a%d" % i, tag="a", bufs=5)
+            a = state["a", i]
+            bank = psum.tile([P, 4, P], F32, name="l%d_%d" % (i, b), tag="mm", bufs=3)
+            blocks = range(4 * b, min(2 * T, 4 * b + 4))
+            for r in blocks:
+                for g in range(2):
+                    nc.tensor.matmul_mx(
+                        out=bank[:, r - 4 * b, :],
+                        lhsT=w2t[:, g, 2 * P * r : 2 * P * (r + 1)].bitcast(FP4X4),
+                        lhsT_scale=w2s[:, g, P * r : P * (r + 1)],
+                        rhs=hq[:, g * P : (g + 1) * P].bitcast(FP8X4),
+                        rhs_scale=hs[:, g * P : (g + 1) * P],
+                        start=(g == 0),
+                        stop=(g == 1),
+                    )
+            for r in blocks:
+                if (i, b) in LOGITS_ON_VECTOR:
+                    nc.vector.tensor_scalar(
+                        out=a[:, r, :], in0=bank[:, r - 4 * b, :], scalar1=b2t[:, r : r + 1], scalar2=None, op0=ALU.add
+                    )
+                else:
+                    nc.scalar.activation(out=a[:, r, :], in_=bank[:, r - 4 * b, :], func=ACT.Identity, bias=b2t[:, r : r + 1])
 
-        def maximum(c, k):
-            h, step = k // 6, k % 6
-            a = state["a", c, h]
+        def maximum(i, step):
+            a = state["a", i]
             if step == 0:
-                state["m", c, h] = work.tile([P, 2, W], F32, name="m%d%d" % (c, h), tag="w", bufs=1)
-                if ("nm", c) not in state:
-                    state["nm", c] = work.tile([P, 2, W], F32, name="nm%d" % c, tag="nm", bufs=2)
-            m = state["m", c, h]
+                state["m", i] = work.tile([P, 8, P], F32, name="m%d" % i, tag="m", bufs=2)
+                state["nm", i] = work.tile([P, 2, P], F32, name="nm%d" % i, tag="nm", bufs=4)
+            m = state["m", i]
             if step == 0:
-                nc.vector.tensor_tensor(out=m[:], in0=a[:, 0:2, :], in1=a[:, 2:4, :], op=ALU.max)
-            elif step < 3:
-                nc.vector.tensor_tensor(out=m[:], in0=m[:], in1=a[:, 2 * step + 2 : 2 * step + 4, :], op=ALU.max)
+                nc.vector.tensor_tensor(out=m[:], in0=a[:, 0:8, :], in1=a[:, 8:16, :], op=ALU.max)
+            elif step == 1:
+                nc.vector.tensor_tensor(out=m[:, 0:4, :], in0=m[:, 0:4, :], in1=m[:, 4:8, :], op=ALU.max)
+            elif step == 2:
+                nc.vector.tensor_tensor(out=m[:, 0:2, :], in0=m[:, 0:2, :], in1=m[:, 2:4, :], op=ALU.max)
             elif step == 3:
-                nc.vector.tensor_tensor(out=m[:, 0, :], in0=m[:, 0, :], in1=m[:, 1, :], op=ALU.max)
-            elif step == 4:
-                nc.vector.tensor_tensor(out=m[:, 0, :], in0=m[:, 0, :], in1=a[:, 8, :], op=ALU.max)
+                nc.vector.tensor_tensor(out=m[:, 0:2, :], in0=m[:, 0:2, :], in1=a[:, 16:18, :], op=ALU.max)
             else:
-                nc.vector.tensor_scalar(
-                    out=state["nm", c][:, h, :], in0=m[:, 0, :], scalar1=-1.0, scalar2=None, op0=ALU.mult
-                )
+                if i in NEGATE_ON_SCALAR:
+                    nc.scalar.activation(out=state["nm", i][:], in_=m[:, 0:2, :], func=ACT.Copy, scale=-1.0)
+                else:
+                    nc.vector.tensor_scalar(
+                        out=state["nm", i][:], in0=m[:, 0:2, :], scalar1=-1.0, scalar2=None, op0=ALU.mult
+                    )
 
         def weights(i, b):
-            c, j = i // 4, i % 4
-            nm = state["nm", c]
-            cols = slice(P * j, P * (j + 1))
+            a, nm = state["a", i], state["nm", i]
             if ("e", i) not in state:
                 state["e", i] = work.tile([P, T, U], F32, name="e%d" % i, tag="e", bufs=3)
                 state["acc", i] = work.tile([P, C, U], F32, name="acc%d" % i, tag="acc", bufs=5)
@@ -270,8 +271,8 @@ def tile_convextapupsampleflowhead_d1p_kernel(
             for t in taps:
                 for h in range(2):
                     dst = d[:, t - 2 * b, h * P : (h + 1) * P]
-                    nc.tensor.matmul(dst, state["a", c, h][:, t, cols], ident[:], start=True, stop=False, is_transpose=True)
-                    nc.tensor.matmul(dst, nm[:, h, cols], ident[:], start=False, stop=True, is_transpose=True)
+                    nc.tensor.matmul(dst, a[:, 2 * t + h, :], ident[:], start=True, stop=False, is_transpose=True)
+                    nc.tensor.matmul(dst, nm[:, h, :], ident[:], start=False, stop=True, is_transpose=True)
             k = len(taps)
             nc.scalar.activation(out=e[:, 2 * b : 2 * b + k, :], in_=d[:, 0:k, :], func=ACT.Exp, scale=0.25)
 
@@ -306,7 +307,7 @@ def tile_convextapupsampleflowhead_d1p_kernel(
             for c in range(C):
                 if (i, c) in SUMS_ON_TENSOR:
                     if ("w", i, c) not in state:
-                        state["w", i, c] = work.tile([P, T, U], F32, name="w%d%d" % (i, c), tag="w", bufs=1)
+                        state["w", i, c] = work.tile([P, T, U], F32, name="w%d%d" % (i, c), tag="w", bufs=3)
                     for t in range(2 * b, min(T, 2 * b + 2)):
                         factor = flow[:, i, C * t + c : C * t + c + 1]
                         dst = state["w", i, c][:, t, :]
@@ -345,7 +346,7 @@ def tile_convextapupsampleflowhead_d1p_kernel(
             e = state["e", i]
             n = GROUP_OF[i]
             if ("ds", n) not in state:
-                state["ds", n] = work.tile([P, U * GROUPS[n]], F32, name="ds%d" % n, tag="ds", bufs=2)
+                state["ds", n] = work.tile([P, U * GROUPS[n]], F32, name="ds%d" % n, tag="ds", bufs=3)
             den = psum.tile([P, 2, P], F32, name="den%d" % i, tag="den", bufs=1)
             for h in range(2):
                 for t in range(T):
@@ -394,7 +395,7 @@ def tile_convextapupsampleflowhead_d1p_kernel(
             state["rd", i] = rd
 
         def finish(i):
-            o = work.tile([P, U, C], F32, name="o%d" % i, tag="o", bufs=2)
+            o = work.tile([P, U, C], F32, name="o%d" % i, tag="o", bufs=3)
             nc.vector.tensor_tensor(
                 out=o[:],
                 in0=state["acc", i][:].rearrange("p c u -> p u c"),
@@ -408,362 +409,364 @@ def tile_convextapupsampleflowhead_d1p_kernel(
                 step(i, *args)
 
         with tc.manual_schedule():
-            widen(0)
             permute(0)
-            widen(1)
+            widen(0)
             turn(0)
-            widen(3)
-            widen(2)
-            turn(3)
-            turn(2)
-            turn(1)
+            widen(1)
+            quant_x(0)
             permute(1)
-            biases()
-            quant_x(0, 0)
-            quant_x(0, 1)
-            hidden(0, 6)
+            turn(1)
+            widen(2)
             hidden(0, 0)
-            hidden(0, 7)
-            widen(4)
-            widen(7)
-            hidden(0, 5)
             hidden(0, 1)
-            widen(5)
-            hidden(0, 4)
-            turn(4)
-            widen(6)
-            turn(7)
-            turn(5)
-            turn(6)
-            hidden(0, 2)
-            hidden(0, 3)
-            gather_h(0, 3)
-            gather_h(0, 2)
-            quant_x(1, 0)
-            quant_x(1, 1)
-            quant_h(0, 1)
-            gather_h(0, 1)
-            hidden(1, 3)
+            quant_x(1)
             gather_h(0, 0)
-            hidden(1, 2)
+            turn(2)
+            biases()
+            widen(3)
+            gather_h(0, 1)
             quant_h(0, 0)
+            quant_h(0, 1)
             hidden(1, 0)
-            hidden(1, 5)
-            hidden(1, 4)
-            hidden(1, 7)
-            hidden(1, 6)
             hidden(1, 1)
-            gather_h(1, 2)
+            quant_x(2)
             gather_h(1, 0)
-            gather_h(1, 3)
-            gather_h(1, 1)
-            quant_h(1, 1)
-            quant_h(1, 0)
+            turn(3)
             logits(0, 3)
-            logits(0, 1)
-            logits(0, 15)
-            logits(0, 4)
             logits(0, 0)
+            widen(4)
+            gather_h(1, 1)
             logits(0, 2)
-            logits(0, 7)
-            logits(0, 5)
-            logits(0, 9)
-            logits(0, 6)
-            logits(0, 10)
-            logits(0, 13)
-            logits(0, 8)
-            logits(0, 12)
-            logits(0, 11)
-            logits(0, 17)
-            logits(0, 14)
-            logits(0, 16)
-            logits(1, 4)
-            logits(1, 3)
-            logits(1, 5)
-            logits(1, 6)
-            logits(1, 1)
-            logits(1, 0)
-            logits(1, 2)
-            logits(1, 11)
-            logits(1, 15)
+            quant_h(1, 0)
+            logits(0, 1)
+            quant_h(1, 1)
+            hidden(2, 0)
             maximum(0, 0)
-            logits(1, 7)
-            logits(1, 12)
-            logits(1, 10)
-            logits(1, 14)
+            hidden(2, 1)
+            quant_x(3)
             maximum(0, 1)
+            logits(0, 4)
             maximum(0, 2)
-            logits(1, 8)
-            logits(1, 9)
+            gather_h(2, 0)
+            turn(4)
             maximum(0, 3)
+            logits(1, 3)
+            logits(1, 0)
+            widen(5)
+            gather_h(2, 1)
             maximum(0, 4)
-            maximum(0, 5)
-            logits(1, 16)
-            maximum(0, 6)
-            maximum(0, 7)
-            maximum(0, 8)
-            maximum(0, 9)
-            maximum(0, 10)
-            maximum(0, 11)
-            logits(1, 13)
-            logits(1, 17)
+            logits(1, 2)
+            quant_h(2, 0)
+            logits(1, 1)
+            quant_h(2, 1)
+            hidden(3, 0)
             maximum(1, 0)
+            hidden(3, 1)
+            quant_x(4)
             maximum(1, 1)
+            logits(1, 4)
             maximum(1, 2)
-            maximum(1, 3)
-            maximum(1, 4)
-            weights(0, 2)
-            maximum(1, 5)
-            maximum(1, 6)
             weights(0, 0)
-            maximum(1, 7)
-            weights(0, 1)
-            first_product(0)
-            weights(0, 3)
+            gather_h(3, 0)
+            turn(5)
+            maximum(1, 3)
+            logits(2, 3)
+            logits(2, 0)
+            widen(6)
+            gather_h(3, 1)
+            maximum(1, 4)
             weights(0, 4)
-            side_products(0, 1)
-            maximum(1, 8)
-            products(0, 3)
-            side_products(0, 2)
-            side_products(0, 0)
-            products(0, 6)
-            weights(1, 2)
-            products(0, 5)
-            denominator(0)
-            side_products(0, 3)
-            maximum(1, 9)
-            weights(1, 0)
-            products(0, 7)
-            side_products(0, 4)
-            inverse(0, 0)
-            weights(1, 1)
-            maximum(1, 10)
-            first_product(1)
-            weights(1, 3)
-            side_sums(0)
-            weights(1, 4)
-            inverse(0, 1)
-            side_products(1, 1)
+            first_product(0)
+            logits(2, 2)
+            quant_h(3, 0)
+            logits(2, 1)
+            weights(0, 1)
+            weights(0, 2)
+            quant_h(3, 1)
+            hidden(4, 0)
             products(0, 1)
-            inverse(0, 2)
-            products(1, 3)
-            side_products(1, 2)
-            products(0, 8)
-            side_products(1, 0)
-            inverse(0, 3)
-            products(1, 6)
-            weights(2, 2)
-            products(0, 2)
-            inverse(0, 4)
-            products(1, 5)
-            denominator(1)
-            inverse(0, 5)
-            side_products(1, 3)
-            weights(2, 0)
+            maximum(2, 0)
+            hidden(4, 1)
+            quant_x(5)
+            maximum(2, 1)
+            logits(2, 4)
             products(0, 4)
-            products(1, 7)
-            inverse(0, 6)
-            side_products(1, 4)
-            inverse(1, 0)
-            weights(2, 1)
-            first_product(2)
-            maximum(1, 11)
-            weights(2, 3)
-            side_sums(1)
-            weights(2, 4)
-            inverse(1, 1)
-            side_products(2, 1)
+            weights(0, 3)
+            maximum(2, 2)
+            weights(1, 0)
+            gather_h(4, 0)
+            turn(6)
+            maximum(2, 3)
+            logits(3, 3)
+            logits(3, 0)
+            widen(7)
+            products(0, 8)
+            gather_h(4, 1)
+            maximum(2, 4)
+            weights(1, 4)
+            denominator(0)
+            products(0, 6)
+            first_product(1)
+            products(0, 2)
+            logits(3, 2)
+            quant_h(4, 0)
+            logits(3, 1)
+            weights(1, 1)
+            products(0, 5)
+            weights(1, 2)
+            products(0, 3)
+            quant_h(4, 1)
+            inverse(0, 0)
+            hidden(5, 0)
             products(1, 1)
-            inverse(1, 2)
-            products(2, 3)
-            side_products(2, 2)
-            products(1, 8)
-            side_products(2, 0)
-            inverse(1, 3)
-            products(2, 6)
-            weights(3, 2)
-            products(1, 2)
-            inverse(1, 4)
-            products(2, 5)
-            denominator(2)
-            inverse(1, 5)
-            side_products(2, 3)
-            weights(3, 0)
+            maximum(3, 0)
+            hidden(5, 1)
+            quant_x(6)
+            inverse(0, 1)
+            maximum(3, 1)
+            logits(3, 4)
             products(1, 4)
-            products(2, 7)
-            inverse(1, 6)
-            side_products(2, 4)
-            inverse(2, 0)
-            weights(3, 1)
-            first_product(3)
-            weights(3, 3)
-            side_sums(2)
-            weights(3, 4)
-            inverse(2, 1)
-            side_products(3, 1)
+            weights(1, 3)
+            maximum(3, 2)
+            weights(2, 0)
+            products(0, 7)
+            gather_h(5, 0)
+            turn(7)
+            maximum(3, 3)
+            logits(4, 3)
+            logits(4, 0)
+            products(1, 8)
+            gather_h(5, 1)
+            maximum(3, 4)
+            weights(2, 4)
+            denominator(1)
+            products(1, 6)
+            first_product(2)
+            inverse(0, 2)
+            products(1, 2)
+            logits(4, 2)
+            quant_h(5, 0)
+            logits(4, 1)
+            weights(2, 1)
+            inverse(0, 3)
+            products(1, 5)
+            weights(2, 2)
+            inverse(0, 4)
+            products(1, 3)
+            quant_h(5, 1)
+            inverse(1, 0)
+            hidden(6, 0)
             products(2, 1)
-            inverse(2, 2)
-            products(3, 3)
-            side_turn(0)
-            side_products(3, 2)
-            products(2, 8)
-            side_products(3, 0)
-            inverse(2, 3)
-            products(3, 6)
-            weights(4, 2)
-            products(2, 2)
-            inverse(2, 4)
-            products(3, 5)
-            denominator(3)
-            inverse(2, 5)
-            side_products(3, 3)
-            weights(4, 0)
+            maximum(4, 0)
+            hidden(6, 1)
+            quant_x(7)
+            inverse(0, 5)
+            inverse(1, 1)
+            maximum(4, 1)
+            inverse(0, 6)
+            logits(4, 4)
             products(2, 4)
-            products(3, 7)
-            inverse(2, 6)
-            side_products(3, 4)
-            inverse(3, 0)
-            weights(4, 1)
-            turn_inverse(0)
-            finish(0)
-            first_product(4)
-            weights(4, 3)
-            side_sums(3)
-            weights(4, 4)
-            inverse(3, 1)
-            side_products(4, 1)
+            weights(2, 3)
+            maximum(4, 2)
+            weights(3, 0)
+            products(1, 7)
+            gather_h(6, 0)
+            maximum(4, 3)
+            logits(5, 3)
+            logits(5, 0)
+            products(2, 8)
+            gather_h(6, 1)
+            maximum(4, 4)
+            weights(3, 4)
+            denominator(2)
+            products(2, 6)
+            first_product(3)
+            inverse(1, 2)
+            products(2, 2)
+            logits(5, 2)
+            quant_h(6, 0)
+            logits(5, 1)
+            weights(3, 1)
+            inverse(1, 3)
+            products(2, 5)
+            weights(3, 2)
+            inverse(1, 4)
+            products(2, 3)
+            quant_h(6, 1)
+            inverse(2, 0)
+            hidden(7, 0)
             products(3, 1)
-            inverse(3, 2)
-            products(4, 3)
-            side_turn(1)
-            side_products(4, 2)
-            products(3, 8)
-            side_products(4, 0)
-            inverse(3, 3)
-            products(4, 6)
-            weights(5, 2)
-            products(3, 2)
-            inverse(3, 4)
-            products(4, 5)
-            denominator(4)
-            inverse(3, 5)
-            side_products(4, 3)
-            weights(5, 0)
+            maximum(5, 0)
+            hidden(7, 1)
+            inverse(1, 5)
+            inverse(2, 1)
+            maximum(5, 1)
+            inverse(1, 6)
+            logits(5, 4)
             products(3, 4)
-            products(4, 7)
-            inverse(3, 6)
-            side_products(4, 4)
-            inverse(4, 0)
-            weights(5, 1)
-            turn_inverse(1)
-            finish(1)
-            first_product(5)
-            weights(5, 3)
-            side_sums(4)
-            weights(5, 4)
-            inverse(4, 1)
-            side_products(5, 1)
+            weights(3, 3)
+            maximum(5, 2)
+            weights(4, 0)
+            products(2, 7)
+            gather_h(7, 0)
+            maximum(5, 3)
+            logits(6, 3)
+            logits(6, 0)
+            products(3, 8)
+            gather_h(7, 1)
+            maximum(5, 4)
+            weights(4, 4)
+            denominator(3)
+            products(3, 6)
+            first_product(4)
+            turn_inverse(0)
+            inverse(2, 2)
+            products(3, 2)
+            logits(6, 2)
+            quant_h(7, 0)
+            logits(6, 1)
+            weights(4, 1)
+            finish(0)
+            inverse(2, 3)
+            products(3, 5)
+            weights(4, 2)
+            inverse(2, 4)
+            products(3, 3)
+            quant_h(7, 1)
+            inverse(3, 0)
             products(4, 1)
-            inverse(4, 2)
-            products(5, 3)
-            side_turn(2)
-            side_products(5, 2)
-            products(4, 8)
-            side_products(5, 0)
-            inverse(4, 3)
-            products(5, 6)
-            weights(6, 2)
-            products(4, 2)
-            inverse(4, 4)
-            products(5, 5)
-            denominator(5)
-            inverse(4, 5)
-            side_products(5, 3)
-            weights(6, 0)
+            maximum(6, 0)
+            inverse(2, 5)
+            inverse(3, 1)
+            maximum(6, 1)
+            inverse(2, 6)
+            logits(6, 4)
             products(4, 4)
-            products(5, 7)
-            inverse(4, 6)
-            side_products(5, 4)
-            inverse(5, 0)
-            weights(6, 1)
-            turn_inverse(2)
-            finish(2)
-            first_product(6)
-            weights(6, 3)
-            side_sums(5)
-            weights(6, 4)
-            inverse(5, 1)
-            side_products(6, 1)
+            weights(4, 3)
+            maximum(6, 2)
+            weights(5, 0)
+            products(3, 7)
+            maximum(6, 3)
+            logits(7, 3)
+            logits(7, 0)
+            products(4, 8)
+            maximum(6, 4)
+            weights(5, 4)
+            denominator(4)
+            products(4, 6)
+            first_product(5)
+            turn_inverse(1)
+            inverse(3, 2)
+            products(4, 2)
+            logits(7, 2)
+            logits(7, 1)
+            weights(5, 1)
+            finish(1)
+            inverse(3, 3)
+            products(4, 5)
+            weights(5, 2)
+            inverse(3, 4)
+            products(4, 3)
+            inverse(4, 0)
             products(5, 1)
-            inverse(5, 2)
-            products(6, 3)
-            side_turn(3)
-            side_products(6, 2)
-            products(5, 8)
-            side_products(6, 0)
-            inverse(5, 3)
-            products(6, 6)
-            weights(7, 2)
-            products(5, 2)
-            inverse(5, 4)
-            products(6, 5)
-            denominator(6)
-            inverse(5, 5)
-            side_products(6, 3)
-            weights(7, 0)
+            maximum(7, 0)
+            inverse(3, 5)
+            inverse(4, 1)
+            maximum(7, 1)
+            inverse(3, 6)
+            logits(7, 4)
             products(5, 4)
-            products(6, 7)
-            inverse(5, 6)
-            side_products(6, 4)
-            inverse(6, 0)
-            weights(7, 1)
-            turn_inverse(3)
-            finish(3)
-            first_product(7)
-            weights(7, 3)
-            side_sums(6)
-            weights(7, 4)
-            inverse(6, 1)
-            side_products(7, 1)
+            weights(5, 3)
+            maximum(7, 2)
+            weights(6, 0)
+            products(4, 7)
+            side_products(6, 0)
+            maximum(7, 3)
+            products(5, 8)
+            maximum(7, 4)
+            weights(6, 4)
+            denominator(5)
+            products(5, 6)
+            first_product(6)
+            turn_inverse(2)
+            inverse(4, 2)
+            products(5, 2)
+            weights(6, 1)
+            finish(2)
+            inverse(4, 3)
+            products(5, 5)
+            weights(6, 2)
+            inverse(4, 4)
+            products(5, 3)
+            inverse(5, 0)
             products(6, 1)
-            inverse(6, 2)
-            products(7, 3)
-            side_turn(4)
-            side_products(7, 2)
-            products(6, 8)
-            side_products(7, 0)
-            inverse(6, 3)
-            products(7, 6)
-            products(6, 2)
-            inverse(6, 4)
-            products(7, 5)
-            denominator(7)
-            inverse(6, 5)
-            side_products(7, 3)
+            inverse(4, 5)
+            inverse(5, 1)
+            inverse(4, 6)
             products(6, 4)
-            products(7, 7)
-            inverse(6, 6)
-            side_products(7, 4)
-            inverse(7, 0)
-            turn_inverse(4)
-            finish(4)
-            side_sums(7)
-            inverse(7, 1)
+            weights(6, 3)
+            side_products(6, 1)
+            weights(7, 0)
+            products(5, 7)
+            side_products(6, 2)
+            side_products(7, 0)
+            side_products(6, 4)
+            products(6, 8)
+            weights(7, 4)
+            denominator(6)
+            side_products(6, 3)
+            products(6, 6)
+            first_product(7)
+            turn_inverse(3)
+            inverse(5, 2)
+            products(6, 2)
+            weights(7, 1)
+            finish(3)
+            inverse(5, 3)
+            products(6, 5)
+            weights(7, 2)
+            inverse(5, 4)
+            products(6, 3)
+            inverse(6, 0)
             products(7, 1)
-            inverse(7, 2)
-            side_turn(5)
+            inverse(5, 5)
+            inverse(6, 1)
+            inverse(5, 6)
+            products(7, 4)
+            side_sums(6)
+            weights(7, 3)
+            side_products(7, 1)
+            products(6, 7)
+            side_products(7, 2)
+            side_products(7, 4)
+            side_turn(6)
             products(7, 8)
-            inverse(7, 3)
+            denominator(7)
+            side_products(7, 3)
+            products(7, 6)
+            turn_inverse(4)
+            inverse(6, 2)
             products(7, 2)
+            finish(4)
+            inverse(6, 3)
+            products(7, 5)
+            inverse(6, 4)
+            products(7, 3)
+            inverse(7, 0)
+            inverse(6, 5)
+            inverse(7, 1)
+            inverse(6, 6)
+            side_sums(7)
+            products(7, 7)
+            side_turn(7)
+            turn_inverse(5)
+            inverse(7, 2)
+            finish(5)
+            inverse(7, 3)
             inverse(7, 4)
             inverse(7, 5)
-            products(7, 4)
             inverse(7, 6)
-            turn_inverse(5)
-            finish(5)
-            side_turn(6)
             turn_inverse(6)
             finish(6)
-            side_turn(7)
             turn_inverse(7)
             finish(7)

@@ -19,18 +19,23 @@ ALU = mybir.AluOpType
 ACT = mybir.ActivationFunctionType
 
 P = 128
+W = 512
+WIDE_HIDDEN_ON_VECTOR = {(1, 1)}
+WIDE_LOGITS_ON_VECTOR = {-1}
+WIDE_GATHER_ON_SCALAR = {-1}
+WIDE_NEGATE_ON_SCALAR = {(1, 1)}
 GROUPS = [2, 2, 2, 1, 1]
 GROUP_OF = [0, 0, 1, 1, 2, 2, 3, 4]
 PLACE_OF = [0, 1, 0, 1, 0, 1, 0, 0]
-HIDDEN_ON_VECTOR = {-1}
-LOGITS_ON_VECTOR = {(0, 1), (0, 0), (0, 3), (0, 2), (1, 1), (1, 0), (1, 3), (1, 2)}
-SUMS_ON_TENSOR = {(6, 1), (7, 1)}
-WIDEN_ON_VECTOR = {2: 4, 3: 4, 6: 4, 7: 4}
-FIRST_ON_VECTOR = {0}
-TURN_ON_VECTOR = {2}
-SIDE_ON_VECTOR = {(7, 0)}
-GATHER_ON_SCALAR = {(1, 1), (2, 0), (2, 1), (5, 1), (6, 1), (7, 1)}
-NEGATE_ON_SCALAR = {0, 3, 6}
+HIDDEN_ON_VECTOR = {(1, 1), (3, 1)}
+LOGITS_ON_VECTOR = {(2, 2), (3, 0)}
+SUMS_ON_TENSOR = {(5, 1), (6, 1), (7, 1)}
+WIDEN_ON_VECTOR = {3: 4, 6: 4, 4: 4, 7: 4}
+FIRST_ON_VECTOR = {6}
+TURN_ON_VECTOR = {2, 3, 4}
+SIDE_ON_VECTOR = {-1}
+GATHER_ON_SCALAR = {-1}
+NEGATE_ON_SCALAR = {3}
 NTILES = N // P
 
 
@@ -120,7 +125,7 @@ def tile_convextapupsampleflowhead_d1p_kernel(
         def biases():
             nc.gpsimd.tensor_copy(out=b2f[:], in_=b2rows[:])
             nc.gpsimd.tensor_scalar(out=flow[:], in0=nbt[:], scalar1=16.0, scalar2=0.0, op0=ALU.mult, op1=ALU.add)
-            b2ps = psum.tile([P, 512], F32, name="b2ps", tag="rd", bufs=1)
+            b2ps = psum.tile([P, 512], F32, name="b2ps", tag="bank", bufs=8)
             nc.tensor.transpose(b2ps[:, 0:P], b2f[:], ident[:])
             nc.scalar.copy(out=b2t[:], in_=b2ps[:, 0 : 2 * T])
 
@@ -128,7 +133,7 @@ def tile_convextapupsampleflowhead_d1p_kernel(
         state = {}
 
         def widen(i):
-            xw = work.tile([P, D], BF16, name="xw%d" % i, tag="xw", bufs=4, align_bytes=64)
+            xw = work.tile([P, D], BF16, name="xw%d" % i, tag="xw", bufs=3, align_bytes=64)
             for k in range(8):
                 block = slice(P * k, P * (k + 1))
                 if k < WIDEN_ON_VECTOR.get(i, 0):
@@ -147,33 +152,39 @@ def tile_convextapupsampleflowhead_d1p_kernel(
 
         def turn(i):
             words = state["xw", i][:].bitcast(F32)
-            xt = psum.tile([P, 2, 2, P], F32, name="xt%d" % i, tag="mm", bufs=3)
+            xt = psum.tile([P, 2, 2, P], F32, name="xt%d" % i, tag="bank", bufs=8)
             for g in range(2):
                 for u in range(2):
                     nc.tensor.transpose(xt[:, g, u, :], words[:, 256 * g + u : 256 * (g + 1) : 2], ident[:])
-            xg = work.tile([P, 2, P, 4], BF16, name="xg%d" % i, tag="xg", bufs=3, align_bytes=64)
-            dst = xg[:].rearrange("p g r e -> p g (r e)").bitcast(F32).rearrange("p g (r u) -> p g r u", u=2)
+            if i < 4:
+                xg = work.tile([P, 2, P, 4], BF16, name="xg%d" % i, tag="xg", bufs=2, align_bytes=64)
+                state["xg", i] = xg
+                region = xg[:]
+            else:
+                if ("xgw", 1) not in state:
+                    state["xgw", 1] = work.tile([P, 2, W, 4], BF16, name="xgw", tag="xgw", bufs=1, align_bytes=64)
+                region = state["xgw", 1][:, :, P * (i - 4) : P * (i - 3), :]
+            dst = region.rearrange("p g r e -> p g (r e)").bitcast(F32).rearrange("p g (r u) -> p g r u", u=2)
             src = xt[:].rearrange("p g u r -> p g r u")
             if i in TURN_ON_VECTOR:
                 nc.vector.tensor_copy(out=dst, in_=src)
             else:
                 nc.scalar.copy(out=dst, in_=src)
-            state["xg", i] = xg
 
         def quant_x(i):
-            xq = work.tile([P, 2 * P], U32, name="xq%d" % i, tag="xq", bufs=3, align_bytes=64)
-            xs = work.tile([P, 2 * P], U8, name="xs%d" % i, tag="xs", bufs=3, align_bytes=64)
+            xq = work.tile([P, 2 * P], U32, name="xq%d" % i, tag="xq", bufs=2, align_bytes=64)
+            xs = work.tile([P, 2 * P], U8, name="xs%d" % i, tag="xs", bufs=2, align_bytes=64)
             nc.vector.quantize_mx(
                 out=xq[:].bitcast(FP8X4), scales=xs[:], in_=state["xg", i][:].rearrange("p g n t -> p (g n t)")
             )
-            hq = work.tile([P, 2 * P], U32, name="hq%d" % i, tag="hq", bufs=5, align_bytes=64)
-            hs = work.tile([P, 2 * P], U8, name="hs%d" % i, tag="hs", bufs=5, align_bytes=64)
+            hq = work.tile([P, 2 * P], U32, name="hq%d" % i, tag="hq", bufs=4, align_bytes=64)
+            hs = work.tile([P, 2 * P], U8, name="hs%d" % i, tag="hs", bufs=4, align_bytes=64)
             state["x", i] = (xq, xs)
             state["h", i] = (hq, hs)
 
         def hidden(i, q):
             xq, xs = state["x", i]
-            bank = psum.tile([P, 4, P], F32, name="h%d%d" % (i, q), tag="mm", bufs=3)
+            bank = psum.tile([P, 4, P], F32, name="h%d%d" % (i, q), tag="bank", bufs=8)
             for t in range(4):
                 for g in range(2):
                     nc.tensor.matmul_mx(
@@ -185,7 +196,7 @@ def tile_convextapupsampleflowhead_d1p_kernel(
                         start=(g == 0),
                         stop=(g == 1),
                     )
-            hr = work.tile([P, 4, P], BF16, name="hr%d%d" % (i, q), tag="hr", bufs=4, align_bytes=64)
+            hr = work.tile([P, 4, P], BF16, name="hr%d%d" % (i, q), tag="hr", bufs=3, align_bytes=64)
             for t in range(4):
                 if (i, q) in HIDDEN_ON_VECTOR:
                     nc.vector.tensor_scalar(
@@ -196,7 +207,7 @@ def tile_convextapupsampleflowhead_d1p_kernel(
             state["hr", i, q] = hr
 
         def gather_h(i, q):
-            hg = work.tile([P, P, 4], BF16, name="hg%d%d" % (i, q), tag="hg", bufs=4, align_bytes=64)
+            hg = work.tile([P, P, 4], BF16, name="hg%d%d" % (i, q), tag="hg", bufs=3, align_bytes=64)
             src = state["hr", i, q][:].rearrange("p t n -> p n t")
             if (i, q) in GATHER_ON_SCALAR:
                 nc.scalar.copy(out=hg[:], in_=src)
@@ -215,9 +226,9 @@ def tile_convextapupsampleflowhead_d1p_kernel(
         def logits(i, b):
             hq, hs = state["h", i]
             if ("a", i) not in state:
-                state["a", i] = work.tile([P, 2 * T, P], F32, name="a%d" % i, tag="a", bufs=5)
+                state["a", i] = work.tile([P, 2 * T, P], F32, name="a%d" % i, tag="a", bufs=3)
             a = state["a", i]
-            bank = psum.tile([P, 4, P], F32, name="l%d_%d" % (i, b), tag="mm", bufs=3)
+            bank = psum.tile([P, 4, P], F32, name="l%d_%d" % (i, b), tag="bank", bufs=8)
             blocks = range(4 * b, min(2 * T, 4 * b + 4))
             for r in blocks:
                 for g in range(2):
@@ -241,8 +252,8 @@ def tile_convextapupsampleflowhead_d1p_kernel(
         def maximum(i, step):
             a = state["a", i]
             if step == 0:
-                state["m", i] = work.tile([P, 8, P], F32, name="m%d" % i, tag="m", bufs=2)
-                state["nm", i] = work.tile([P, 2, P], F32, name="nm%d" % i, tag="nm", bufs=4)
+                state["m", i] = work.tile([P, 8, P], F32, name="m%d" % i, tag="m", bufs=1)
+                state["nm", i] = work.tile([P, 2, P], F32, name="nm%d" % i, tag="nm", bufs=3)
             m = state["m", i]
             if step == 0:
                 nc.vector.tensor_tensor(out=m[:], in0=a[:, 0:8, :], in1=a[:, 8:16, :], op=ALU.max)
@@ -260,19 +271,127 @@ def tile_convextapupsampleflowhead_d1p_kernel(
                         out=state["nm", i][:], in0=m[:, 0:2, :], scalar1=-1.0, scalar2=None, op0=ALU.mult
                     )
 
+        def quant_x_w(c, g):
+            if ("xqw", c) not in state:
+                state["xqw", c] = work.tile([P, 2, W], U32, name="xqw%d" % c, tag="xqw", bufs=1, align_bytes=64)
+                state["xsw", c] = work.tile([P, 2, W], U8, name="xsw%d" % c, tag="xsw", bufs=1, align_bytes=64)
+            nc.vector.quantize_mx(
+                out=state["xqw", c][:, g, :].bitcast(FP8X4),
+                scales=state["xsw", c][:, g, :],
+                in_=state["xgw", c][:, g, :, :].rearrange("p n t -> p (n t)"),
+            )
+
+        def hidden_w(c, k):
+            q, t = k // 4, k % 4
+            xq, xs = state["xqw", c], state["xsw", c]
+            if ("hrw", c, q) not in state:
+                state["hrw", c, q] = work.tile([P, 4, W], BF16, name="hrw%d%d" % (c, q), tag="hrw", bufs=2, align_bytes=64)
+            bank = psum.tile([P, W], F32, name="hw%d_%d" % (c, k), tag="bank", bufs=8)
+            for g in range(2):
+                nc.tensor.matmul_mx(
+                    out=bank[:],
+                    lhsT=w1p[:, g, q, t, :].bitcast(FP4X4),
+                    lhsT_scale=w1sp[:, g, q, t, :],
+                    rhs=xq[:, g, :].bitcast(FP8X4),
+                    rhs_scale=xs[:, g, :],
+                    start=(g == 0),
+                    stop=(g == 1),
+                )
+            if (c, k) in WIDE_HIDDEN_ON_VECTOR:
+                nc.vector.tensor_scalar(
+                    out=state["hrw", c, q][:, t, :], in0=bank[:], scalar1=b1t[:, q, t : t + 1], scalar2=0.0, op0=ALU.add, op1=ALU.max
+                )
+            else:
+                nc.scalar.activation(out=state["hrw", c, q][:, t, :], in_=bank[:], func=ACT.Relu, bias=b1t[:, q, t : t + 1])
+
+        def gather_h_w(c, k):
+            q, part = k // 2, k % 2
+            if ("hgw", c, q) not in state:
+                state["hgw", c, q] = work.tile([P, W, 4], BF16, name="hgw%d%d" % (c, q), tag="hgw", bufs=1, align_bytes=64)
+            cols = slice(256 * part, 256 * (part + 1))
+            dst, src = state["hgw", c, q][:, cols, :], state["hrw", c, q][:, :, cols].rearrange("p t n -> p n t")
+            if (c, k) in WIDE_GATHER_ON_SCALAR:
+                nc.scalar.copy(out=dst, in_=src)
+            else:
+                nc.vector.tensor_copy(out=dst, in_=src)
+
+        def quant_h_w(c, q):
+            if ("hqw", c) not in state:
+                state["hqw", c] = work.tile([P, 2, W], U32, name="hqw%d" % c, tag="hqw", bufs=1, align_bytes=64)
+                state["hsw", c] = work.tile([P, 2, W], U8, name="hsw%d" % c, tag="hsw", bufs=1, align_bytes=64)
+            nc.vector.quantize_mx(
+                out=state["hqw", c][:, q, :].bitcast(FP8X4),
+                scales=state["hsw", c][:, q, :],
+                in_=state["hgw", c, q][:].rearrange("p n t -> p (n t)"),
+            )
+
+        def logits_w(c, k):
+            h, t = k // T, k % T
+            hq, hs = state["hqw", c], state["hsw", c]
+            if ("aw", c, h) not in state:
+                state["aw", c, h] = work.tile([P, T, W], F32, name="aw%d%d" % (c, h), tag="aw%d" % h, bufs=1)
+            col = U * t + P * h
+            bank = psum.tile([P, W], F32, name="lw%d_%d" % (c, k), tag="bank", bufs=8)
+            for g in range(2):
+                nc.tensor.matmul_mx(
+                    out=bank[:],
+                    lhsT=w2t[:, g, 2 * col : 2 * (col + P)].bitcast(FP4X4),
+                    lhsT_scale=w2s[:, g, col : col + P],
+                    rhs=hq[:, g, :].bitcast(FP8X4),
+                    rhs_scale=hs[:, g, :],
+                    start=(g == 0),
+                    stop=(g == 1),
+                )
+            bias = b2t[:, 2 * t + h : 2 * t + h + 1]
+            if (c, k) in WIDE_LOGITS_ON_VECTOR:
+                nc.vector.tensor_scalar(out=state["aw", c, h][:, t, :], in0=bank[:], scalar1=bias, scalar2=None, op0=ALU.add)
+            else:
+                nc.scalar.activation(out=state["aw", c, h][:, t, :], in_=bank[:], func=ACT.Identity, bias=bias)
+
+        def maximum_w(c, k):
+            h, step = k // 6, k % 6
+            a = state["aw", c, h]
+            if step == 0:
+                state["mw", c, h] = work.tile([P, 2, W], F32, name="mw%d%d" % (c, h), tag="mw", bufs=1)
+                if ("nmw", c) not in state:
+                    state["nmw", c] = work.tile([P, 2, W], F32, name="nmw%d" % c, tag="nmw", bufs=1)
+            m = state["mw", c, h]
+            if step == 0:
+                nc.vector.tensor_tensor(out=m[:], in0=a[:, 0:2, :], in1=a[:, 2:4, :], op=ALU.max)
+            elif step < 3:
+                nc.vector.tensor_tensor(out=m[:], in0=m[:], in1=a[:, 2 * step + 2 : 2 * step + 4, :], op=ALU.max)
+            elif step == 3:
+                nc.vector.tensor_tensor(out=m[:, 0, :], in0=m[:, 0, :], in1=m[:, 1, :], op=ALU.max)
+            elif step == 4:
+                nc.vector.tensor_tensor(out=m[:, 0, :], in0=m[:, 0, :], in1=a[:, 8, :], op=ALU.max)
+            else:
+                if (c, h) in WIDE_NEGATE_ON_SCALAR:
+                    nc.scalar.activation(out=state["nmw", c][:, h, :], in_=m[:, 0, :], func=ACT.Copy, scale=-1.0)
+                else:
+                    nc.vector.tensor_scalar(
+                        out=state["nmw", c][:, h, :], in0=m[:, 0, :], scalar1=-1.0, scalar2=None, op0=ALU.mult
+                    )
+
         def weights(i, b):
-            a, nm = state["a", i], state["nm", i]
+            if i < 4:
+                a = [state["a", i][:, h : 2 * T : 2, :] for h in range(2)]
+                nm = state["nm", i]
+                cols = slice(0, P)
+            else:
+                a = [state["aw", 1, h] for h in range(2)]
+                nm = state["nmw", 1]
+                cols = slice(P * (i - 4), P * (i - 3))
             if ("e", i) not in state:
                 state["e", i] = work.tile([P, T, U], F32, name="e%d" % i, tag="e", bufs=3)
                 state["acc", i] = work.tile([P, C, U], F32, name="acc%d" % i, tag="acc", bufs=5)
             e = state["e", i]
             taps = range(2 * b, min(T, 2 * b + 2))
-            d = psum.tile([P, 2, U], F32, name="d%d_%d" % (i, b), tag="d", bufs=3)
+            d = psum.tile([P, 2, U], F32, name="d%d_%d" % (i, b), tag="bank", bufs=8)
             for t in taps:
                 for h in range(2):
                     dst = d[:, t - 2 * b, h * P : (h + 1) * P]
-                    nc.tensor.matmul(dst, a[:, 2 * t + h, :], ident[:], start=True, stop=False, is_transpose=True)
-                    nc.tensor.matmul(dst, nm[:, h, :], ident[:], start=False, stop=True, is_transpose=True)
+                    nc.tensor.matmul(dst, a[h][:, t, cols], ident[:], start=True, stop=False, is_transpose=True)
+                    nc.tensor.matmul(dst, nm[:, h, cols], ident[:], start=False, stop=True, is_transpose=True)
             k = len(taps)
             nc.scalar.activation(out=e[:, 2 * b : 2 * b + k, :], in_=d[:, 0:k, :], func=ACT.Exp, scale=0.25)
 
@@ -307,7 +426,7 @@ def tile_convextapupsampleflowhead_d1p_kernel(
             for c in range(C):
                 if (i, c) in SUMS_ON_TENSOR:
                     if ("w", i, c) not in state:
-                        state["w", i, c] = work.tile([P, T, U], F32, name="w%d%d" % (i, c), tag="w", bufs=3)
+                        state["w", i, c] = work.tile([P, T, U], F32, name="w%d%d" % (i, c), tag="a", bufs=3)
                     for t in range(2 * b, min(T, 2 * b + 2)):
                         factor = flow[:, i, C * t + c : C * t + c + 1]
                         dst = state["w", i, c][:, t, :]
@@ -319,7 +438,7 @@ def tile_convextapupsampleflowhead_d1p_kernel(
         def side_sums(i):
             for c in range(C):
                 if (i, c) in SUMS_ON_TENSOR:
-                    bank = psum.tile([P, 512], F32, name="sum%d%d" % (i, c), tag="den", bufs=1)
+                    bank = psum.tile([P, 512], F32, name="sum%d%d" % (i, c), tag="bank", bufs=8)
                     for h in range(2):
                         for t in range(T):
                             nc.tensor.matmul(
@@ -330,14 +449,14 @@ def tile_convextapupsampleflowhead_d1p_kernel(
                                 stop=(t == T - 1),
                                 is_transpose=True,
                             )
-                    sums = work.tile([P, 2, P], F32, name="sums%d%d" % (i, c), tag="sums", bufs=4)
+                    sums = work.tile([P, 2, P], F32, name="sums%d%d" % (i, c), tag="sums", bufs=3)
                     nc.scalar.copy(out=sums[:].rearrange("p h n -> p (h n)"), in_=bank[:, 0:U])
                     state["sums", i, c] = sums
 
         def side_turn(i):
             for c in range(C):
                 if (i, c) in SUMS_ON_TENSOR:
-                    bank = psum.tile([P, 512], F32, name="back%d%d" % (i, c), tag="rd", bufs=1)
+                    bank = psum.tile([P, 512], F32, name="back%d%d" % (i, c), tag="bank", bufs=8)
                     for h in range(2):
                         nc.tensor.transpose(bank[:, h * P : (h + 1) * P], state["sums", i, c][:, h, :], ident[:])
                     nc.scalar.copy(out=state["acc", i][:, c, :], in_=bank[:, 0:U])
@@ -346,8 +465,8 @@ def tile_convextapupsampleflowhead_d1p_kernel(
             e = state["e", i]
             n = GROUP_OF[i]
             if ("ds", n) not in state:
-                state["ds", n] = work.tile([P, U * GROUPS[n]], F32, name="ds%d" % n, tag="ds", bufs=3)
-            den = psum.tile([P, 2, P], F32, name="den%d" % i, tag="den", bufs=1)
+                state["ds", n] = work.tile([P, U * GROUPS[n]], F32, name="ds%d" % n, tag="ds", bufs=2)
+            den = psum.tile([P, 2, P], F32, name="den%d" % i, tag="bank", bufs=8)
             for h in range(2):
                 for t in range(T):
                     nc.tensor.matmul(
@@ -388,7 +507,7 @@ def tile_convextapupsampleflowhead_d1p_kernel(
 
         def turn_inverse(i):
             n = GROUP_OF[i]
-            rd = psum.tile([P, 512], F32, name="rd%d" % i, tag="rd", bufs=1)
+            rd = psum.tile([P, 512], F32, name="rd%d" % i, tag="bank", bufs=8)
             for h in range(2):
                 at = U * PLACE_OF[i] + P * h
                 nc.tensor.transpose(rd[:, h * P : (h + 1) * P], state["inv", n][:, at : at + P], ident[:])
@@ -410,363 +529,348 @@ def tile_convextapupsampleflowhead_d1p_kernel(
 
         with tc.manual_schedule():
             permute(0)
-            widen(0)
-            turn(0)
-            widen(1)
-            quant_x(0)
             permute(1)
-            turn(1)
+            widen(0)
+            widen(1)
+            turn(0)
+            quant_x(0)
             widen(2)
-            hidden(0, 0)
-            hidden(0, 1)
+            turn(1)
             quant_x(1)
-            gather_h(0, 0)
-            turn(2)
-            biases()
+            hidden(0, 1)
             widen(3)
-            gather_h(0, 1)
-            quant_h(0, 0)
-            quant_h(0, 1)
-            hidden(1, 0)
-            hidden(1, 1)
-            quant_x(2)
-            gather_h(1, 0)
-            turn(3)
-            logits(0, 3)
-            logits(0, 0)
+            hidden(0, 0)
+            turn(2)
             widen(4)
-            gather_h(1, 1)
-            logits(0, 2)
-            quant_h(1, 0)
-            logits(0, 1)
-            quant_h(1, 1)
-            hidden(2, 0)
-            maximum(0, 0)
-            hidden(2, 1)
+            quant_x(2)
+            gather_h(0, 1)
+            quant_h(0, 1)
+            widen(7)
+            hidden(1, 1)
+            hidden(1, 0)
+            turn(3)
+            widen(6)
+            gather_h(0, 0)
             quant_x(3)
-            maximum(0, 1)
-            logits(0, 4)
-            maximum(0, 2)
-            gather_h(2, 0)
+            gather_h(1, 1)
             turn(4)
-            maximum(0, 3)
-            logits(1, 3)
-            logits(1, 0)
+            quant_h(1, 1)
             widen(5)
+            quant_h(0, 0)
+            hidden(2, 1)
+            hidden(2, 0)
+            gather_h(1, 0)
+            turn(7)
             gather_h(2, 1)
-            maximum(0, 4)
-            logits(1, 2)
-            quant_h(2, 0)
-            logits(1, 1)
-            quant_h(2, 1)
-            hidden(3, 0)
-            maximum(1, 0)
-            hidden(3, 1)
-            quant_x(4)
-            maximum(1, 1)
-            logits(1, 4)
-            maximum(1, 2)
-            weights(0, 0)
-            gather_h(3, 0)
+            turn(6)
+            biases()
             turn(5)
+            quant_h(2, 1)
+            quant_h(1, 0)
+            hidden(3, 1)
+            hidden(3, 0)
+            gather_h(2, 0)
+            gather_h(3, 1)
+            quant_x_w(1, 0)
+            quant_h(3, 1)
+            quant_x_w(1, 1)
+            quant_h(2, 0)
+            gather_h(3, 0)
+            quant_h(3, 0)
+            logits(0, 0)
+            logits(0, 3)
+            logits(0, 1)
+            logits(0, 2)
+            logits(0, 4)
+            hidden_w(1, 0)
+            maximum(0, 0)
+            maximum(0, 1)
+            hidden_w(1, 3)
+            hidden_w(1, 1)
+            maximum(0, 2)
+            logits(1, 0)
+            maximum(0, 3)
+            hidden_w(1, 2)
+            logits(1, 3)
+            logits(1, 1)
+            logits(1, 2)
+            gather_h_w(1, 0)
+            hidden_w(1, 4)
+            hidden_w(1, 7)
+            maximum(0, 4)
+            hidden_w(1, 6)
+            gather_h_w(1, 1)
+            hidden_w(1, 5)
+            logits(1, 4)
+            quant_h_w(1, 0)
+            maximum(1, 0)
+            maximum(1, 1)
+            maximum(1, 2)
+            logits(2, 0)
+            gather_h_w(1, 2)
             maximum(1, 3)
             logits(2, 3)
-            logits(2, 0)
-            widen(6)
-            gather_h(3, 1)
-            maximum(1, 4)
-            weights(0, 4)
-            first_product(0)
-            logits(2, 2)
-            quant_h(3, 0)
             logits(2, 1)
-            weights(0, 1)
-            weights(0, 2)
-            quant_h(3, 1)
-            hidden(4, 0)
-            products(0, 1)
-            maximum(2, 0)
-            hidden(4, 1)
-            quant_x(5)
-            maximum(2, 1)
+            logits(2, 2)
+            maximum(1, 4)
             logits(2, 4)
-            products(0, 4)
+            weights(0, 0)
+            first_product(0)
             weights(0, 3)
+            gather_h_w(1, 3)
+            weights(0, 4)
+            maximum(2, 0)
+            quant_h_w(1, 1)
+            weights(0, 2)
+            maximum(2, 1)
+            weights(0, 1)
             maximum(2, 2)
-            weights(1, 0)
-            gather_h(4, 0)
-            turn(6)
+            logits(3, 0)
             maximum(2, 3)
             logits(3, 3)
-            logits(3, 0)
-            widen(7)
-            products(0, 8)
-            gather_h(4, 1)
-            maximum(2, 4)
-            weights(1, 4)
-            denominator(0)
-            products(0, 6)
-            first_product(1)
-            products(0, 2)
-            logits(3, 2)
-            quant_h(4, 0)
             logits(3, 1)
-            weights(1, 1)
-            products(0, 5)
-            weights(1, 2)
-            products(0, 3)
-            quant_h(4, 1)
-            inverse(0, 0)
-            hidden(5, 0)
-            products(1, 1)
-            maximum(3, 0)
-            hidden(5, 1)
-            quant_x(6)
-            inverse(0, 1)
-            maximum(3, 1)
+            products(0, 1)
+            logits(3, 2)
+            logits_w(1, 0)
+            maximum(2, 4)
+            logits_w(1, 3)
+            products(0, 8)
+            logits_w(1, 2)
+            logits_w(1, 1)
+            logits_w(1, 5)
+            logits_w(1, 4)
             logits(3, 4)
-            products(1, 4)
-            weights(1, 3)
-            maximum(3, 2)
-            weights(2, 0)
+            products(0, 6)
+            logits_w(1, 7)
+            logits_w(1, 6)
+            weights(1, 0)
+            first_product(1)
             products(0, 7)
-            gather_h(5, 0)
-            turn(7)
+            weights(1, 3)
+            weights(1, 4)
+            logits_w(1, 8)
+            maximum(3, 0)
+            logits_w(1, 9)
+            logits_w(1, 10)
+            logits_w(1, 11)
+            logits_w(1, 12)
+            logits_w(1, 14)
+            logits_w(1, 16)
+            logits_w(1, 13)
+            products(0, 5)
+            logits_w(1, 15)
+            weights(1, 2)
+            maximum(3, 1)
+            maximum_w(1, 0)
+            denominator(0)
+            weights(1, 1)
+            maximum(3, 2)
+            maximum_w(1, 1)
             maximum(3, 3)
-            logits(4, 3)
-            logits(4, 0)
-            products(1, 8)
-            gather_h(5, 1)
+            maximum_w(1, 2)
+            products(1, 1)
+            products(0, 2)
+            maximum_w(1, 3)
             maximum(3, 4)
-            weights(2, 4)
-            denominator(1)
+            products(1, 8)
+            maximum_w(1, 4)
             products(1, 6)
+            inverse(0, 0)
+            weights(2, 0)
+            maximum_w(1, 5)
             first_product(2)
-            inverse(0, 2)
-            products(1, 2)
-            logits(4, 2)
-            quant_h(5, 0)
-            logits(4, 1)
-            weights(2, 1)
-            inverse(0, 3)
+            products(1, 7)
+            maximum_w(1, 6)
+            weights(2, 3)
+            weights(2, 4)
+            inverse(0, 1)
+            products(0, 4)
+            maximum_w(1, 7)
             products(1, 5)
             weights(2, 2)
-            inverse(0, 4)
-            products(1, 3)
-            quant_h(5, 1)
-            inverse(1, 0)
-            hidden(6, 0)
+            denominator(1)
+            weights(2, 1)
+            logits_w(1, 17)
+            maximum_w(1, 8)
+            inverse(0, 2)
+            products(0, 3)
+            maximum_w(1, 9)
+            inverse(0, 3)
             products(2, 1)
-            maximum(4, 0)
-            hidden(6, 1)
-            quant_x(7)
-            inverse(0, 5)
-            inverse(1, 1)
-            maximum(4, 1)
-            inverse(0, 6)
-            logits(4, 4)
-            products(2, 4)
-            weights(2, 3)
-            maximum(4, 2)
-            weights(3, 0)
-            products(1, 7)
-            gather_h(6, 0)
-            maximum(4, 3)
-            logits(5, 3)
-            logits(5, 0)
+            products(1, 2)
+            inverse(0, 4)
             products(2, 8)
-            gather_h(6, 1)
-            maximum(4, 4)
-            weights(3, 4)
-            denominator(2)
+            inverse(0, 5)
             products(2, 6)
+            inverse(0, 6)
+            inverse(1, 0)
+            weights(3, 0)
             first_product(3)
-            inverse(1, 2)
-            products(2, 2)
-            logits(5, 2)
-            quant_h(6, 0)
-            logits(5, 1)
-            weights(3, 1)
-            inverse(1, 3)
+            products(2, 7)
+            weights(3, 3)
+            weights(3, 4)
+            inverse(1, 1)
+            products(1, 4)
+            maximum_w(1, 10)
+            maximum_w(1, 11)
             products(2, 5)
             weights(3, 2)
-            inverse(1, 4)
-            products(2, 3)
-            quant_h(6, 1)
-            inverse(2, 0)
-            hidden(7, 0)
+            denominator(2)
+            weights(3, 1)
+            inverse(1, 2)
+            products(1, 3)
+            inverse(1, 3)
             products(3, 1)
-            maximum(5, 0)
-            hidden(7, 1)
-            inverse(1, 5)
-            inverse(2, 1)
-            maximum(5, 1)
-            inverse(1, 6)
-            logits(5, 4)
-            products(3, 4)
-            weights(3, 3)
-            maximum(5, 2)
-            weights(4, 0)
-            products(2, 7)
-            gather_h(7, 0)
-            maximum(5, 3)
-            logits(6, 3)
-            logits(6, 0)
+            products(2, 2)
+            inverse(1, 4)
             products(3, 8)
-            gather_h(7, 1)
-            maximum(5, 4)
-            weights(4, 4)
-            denominator(3)
+            inverse(1, 5)
             products(3, 6)
+            inverse(1, 6)
+            inverse(2, 0)
+            weights(4, 0)
             first_product(4)
-            turn_inverse(0)
-            inverse(2, 2)
-            products(3, 2)
-            logits(6, 2)
-            quant_h(7, 0)
-            logits(6, 1)
-            weights(4, 1)
-            finish(0)
-            inverse(2, 3)
+            products(3, 7)
+            weights(4, 3)
+            weights(4, 4)
+            inverse(2, 1)
+            products(2, 4)
             products(3, 5)
             weights(4, 2)
-            inverse(2, 4)
-            products(3, 3)
-            quant_h(7, 1)
-            inverse(3, 0)
+            denominator(3)
+            weights(4, 1)
+            inverse(2, 2)
+            products(2, 3)
+            inverse(2, 3)
             products(4, 1)
-            maximum(6, 0)
-            inverse(2, 5)
-            inverse(3, 1)
-            maximum(6, 1)
-            inverse(2, 6)
-            logits(6, 4)
-            products(4, 4)
-            weights(4, 3)
-            maximum(6, 2)
-            weights(5, 0)
-            products(3, 7)
-            maximum(6, 3)
-            logits(7, 3)
-            logits(7, 0)
+            products(3, 2)
+            inverse(2, 4)
             products(4, 8)
-            maximum(6, 4)
-            weights(5, 4)
-            denominator(4)
+            turn_inverse(0)
+            finish(0)
+            inverse(2, 5)
             products(4, 6)
+            inverse(2, 6)
+            inverse(3, 0)
+            weights(5, 0)
             first_product(5)
-            turn_inverse(1)
-            inverse(3, 2)
-            products(4, 2)
-            logits(7, 2)
-            logits(7, 1)
-            weights(5, 1)
-            finish(1)
-            inverse(3, 3)
+            products(4, 7)
+            weights(5, 3)
+            weights(5, 4)
+            inverse(3, 1)
+            products(3, 4)
             products(4, 5)
             weights(5, 2)
-            inverse(3, 4)
-            products(4, 3)
-            inverse(4, 0)
+            denominator(4)
+            weights(5, 1)
+            inverse(3, 2)
+            products(3, 3)
+            inverse(3, 3)
             products(5, 1)
-            maximum(7, 0)
-            inverse(3, 5)
-            inverse(4, 1)
-            maximum(7, 1)
-            inverse(3, 6)
-            logits(7, 4)
-            products(5, 4)
-            weights(5, 3)
-            maximum(7, 2)
-            weights(6, 0)
-            products(4, 7)
-            side_products(6, 0)
-            maximum(7, 3)
+            products(4, 2)
+            inverse(3, 4)
+            side_products(5, 2)
             products(5, 8)
-            maximum(7, 4)
-            weights(6, 4)
-            denominator(5)
+            turn_inverse(1)
+            finish(1)
+            side_products(5, 0)
+            inverse(3, 5)
             products(5, 6)
+            inverse(3, 6)
+            inverse(4, 0)
+            weights(6, 0)
             first_product(6)
-            turn_inverse(2)
-            inverse(4, 2)
-            products(5, 2)
-            weights(6, 1)
-            finish(2)
-            inverse(4, 3)
+            products(5, 7)
+            weights(6, 3)
+            weights(6, 4)
+            inverse(4, 1)
+            products(4, 4)
+            side_products(5, 1)
             products(5, 5)
             weights(6, 2)
-            inverse(4, 4)
-            products(5, 3)
-            inverse(5, 0)
+            denominator(5)
+            weights(6, 1)
+            inverse(4, 2)
+            products(4, 3)
+            side_products(5, 3)
+            side_products(5, 4)
+            inverse(4, 3)
             products(6, 1)
-            inverse(4, 5)
-            inverse(5, 1)
-            inverse(4, 6)
-            products(6, 4)
-            weights(6, 3)
-            side_products(6, 1)
-            weights(7, 0)
-            products(5, 7)
+            products(5, 2)
+            inverse(4, 4)
             side_products(6, 2)
-            side_products(7, 0)
-            side_products(6, 4)
             products(6, 8)
-            weights(7, 4)
-            denominator(6)
-            side_products(6, 3)
+            turn_inverse(2)
+            finish(2)
+            side_products(6, 0)
+            inverse(4, 5)
             products(6, 6)
+            inverse(4, 6)
+            inverse(5, 0)
+            weights(7, 0)
             first_product(7)
-            turn_inverse(3)
-            inverse(5, 2)
-            products(6, 2)
-            weights(7, 1)
-            finish(3)
-            inverse(5, 3)
+            products(6, 7)
+            weights(7, 3)
+            weights(7, 4)
+            inverse(5, 1)
+            products(5, 4)
+            side_products(6, 1)
             products(6, 5)
             weights(7, 2)
-            inverse(5, 4)
-            products(6, 3)
-            inverse(6, 0)
+            denominator(6)
+            weights(7, 1)
+            inverse(5, 2)
+            products(5, 3)
+            side_products(6, 3)
+            side_products(6, 4)
+            inverse(5, 3)
             products(7, 1)
+            products(6, 2)
+            inverse(5, 4)
+            side_products(7, 2)
+            products(7, 8)
+            turn_inverse(3)
+            finish(3)
+            side_products(7, 0)
             inverse(5, 5)
-            inverse(6, 1)
+            products(7, 6)
             inverse(5, 6)
+            inverse(6, 0)
+            products(7, 7)
+            inverse(6, 1)
+            products(6, 4)
+            side_sums(5)
+            side_products(7, 1)
+            products(7, 5)
+            denominator(7)
+            inverse(6, 2)
+            products(6, 3)
+            side_products(7, 3)
+            side_products(7, 4)
+            inverse(6, 3)
+            products(7, 2)
+            inverse(6, 4)
+            turn_inverse(4)
+            finish(4)
+            inverse(6, 5)
+            inverse(6, 6)
+            inverse(7, 0)
+            inverse(7, 1)
             products(7, 4)
             side_sums(6)
-            weights(7, 3)
-            side_products(7, 1)
-            products(6, 7)
-            side_products(7, 2)
-            side_products(7, 4)
-            side_turn(6)
-            products(7, 8)
-            denominator(7)
-            side_products(7, 3)
-            products(7, 6)
-            turn_inverse(4)
-            inverse(6, 2)
-            products(7, 2)
-            finish(4)
-            inverse(6, 3)
-            products(7, 5)
-            inverse(6, 4)
-            products(7, 3)
-            inverse(7, 0)
-            inverse(6, 5)
-            inverse(7, 1)
-            inverse(6, 6)
-            side_sums(7)
-            products(7, 7)
-            side_turn(7)
-            turn_inverse(5)
+            side_turn(5)
             inverse(7, 2)
-            finish(5)
+            products(7, 3)
             inverse(7, 3)
             inverse(7, 4)
+            turn_inverse(5)
+            finish(5)
             inverse(7, 5)
             inverse(7, 6)
+            side_sums(7)
+            side_turn(6)
             turn_inverse(6)
             finish(6)
+            side_turn(7)
             turn_inverse(7)
             finish(7)

from contextlib import ExitStack

import concourse.mybir as mybir
from concourse.masks import make_identity

N, D, F, T, U, C = 1024, 1024, 1024, 9, 256, 2
TU = T * U
FLOPS = 2 * N * D * F + 2 * N * F * TU

F32 = mybir.dt.float32
BF16 = mybir.dt.bfloat16
U32 = mybir.dt.uint32
I32 = mybir.dt.int32
U8 = mybir.dt.uint8
FP8 = mybir.dt.float8_e4m3fn
FP8X4 = mybir.dt.float8_e4m3fn_x4
FP4X4 = mybir.dt.float4_e2m1fn_x4
ALU = mybir.AluOpType
ACT = mybir.ActivationFunctionType

P = 128
W = 512
WIDE_HIDDEN_ON_VECTOR = {(1, 1)}
WIDE_LOGITS_ON_VECTOR = {-1}
WIDE_GATHER_ON_SCALAR = {-1}
WIDE_NEGATE_ON_SCALAR = {(1, 1)}
GROUPS = [2, 2, 2, 1, 1]
GROUP_OF = [0, 0, 1, 1, 2, 2, 3, 4]
PLACE_OF = [0, 1, 0, 1, 0, 1, 0, 0]
HIDDEN_ON_VECTOR = {(1, 1), (3, 1)}
LOGITS_ON_VECTOR = {(2, 2), (3, 0)}
SUMS_ON_TENSOR = {(5, 1), (6, 1), (7, 1)}
WIDEN_ON_VECTOR = {3: 4, 6: 4, 4: 4, 7: 4}
FIRST_ON_VECTOR = {6}
TURN_ON_VECTOR = {2, 3, 4}
SIDE_ON_VECTOR = {-1}
GATHER_ON_SCALAR = {-1}
NEGATE_ON_SCALAR = {3}
NTILES = N // P


def tile_convextapupsampleflowhead_d1p_kernel(
    tc, x_bytes, x_scale, w1_words, w1_scales, b1, w2_words, w2_scales, b2, nb, out
):
    nc = tc.nc
    x_view = x_bytes.rearrange("(p i) k -> p i k", i=NTILES)
    out_view = out.rearrange("(p i) u c -> p i (u c)", i=NTILES)

    with ExitStack() as ctx:
        keep = ctx.enter_context(tc.tile_pool(name="keep", bufs=1))
        work = ctx.enter_context(tc.tile_pool(name="work", bufs=2))
        psum = ctx.enter_context(tc.psum_pool(name="psum", bufs=1))

        w1s = keep.tile([P, 2, F], U8, name="w1s", align_bytes=64)
        w2s = keep.tile([P, 2, TU], U8, name="w2s", align_bytes=64)
        nc.vector.memset(w1s[:].bitcast(I32), 0)
        nc.gpsimd.memset(w2s[:].bitcast(I32), 0)
        b2rows = keep.tile([P, P], BF16, name="b2rows")
        nc.gpsimd.memset(b2rows[:], 0.0)

        xsc = keep.tile([P, NTILES, 8], F32, name="xsc")
        nc.sync.dma_start(out=xsc[:], in_=x_scale.rearrange("(p i) j -> p i j", i=NTILES))
        w1t = keep.tile([P, 2, 2 * F], U8, name="w1t", align_bytes=64)
        xb = []
        for i in range(NTILES):
            xbt = keep.tile([P, D], U8, name="xbytes%d" % i, align_bytes=64)
            xb.append(xbt)
        w1_view = w1_words.rearrange("g p n -> p g n")

        def load_x(i):
            nc.sync.dma_start(out=xb[i][:], in_=x_view[:, i, :])

        def load_w1(q):
            half = slice(D * q, D * (q + 1))
            nc.sync.dma_start(out=w1t[:, :, half].bitcast(I32), in_=w1_view[:, :, half].bitcast(I32))

        load_x(0)
        load_w1(0)
        for q in range(4):
            nc.sync.dma_start(
                out=w1s[32 * q : 32 * q + 4, :, :].bitcast(I32),
                in_=w1_scales[:, 4 * q : 4 * q + 4, :].rearrange("g q n -> q g n").bitcast(I32),
            )
        load_x(1)
        load_w1(1)
        load_x(2)
        b1t = keep.tile([P, 2, 4], BF16, name="b1t")
        nc.scalar.dma_start(out=b1t[:], in_=b1.rearrange("(g p t) -> p g t", p=P, t=4))
        nc.scalar.dma_start(out=b2rows[0 : 2 * T, :], in_=b2.rearrange("(r u) -> r u", u=P))
        nbt = keep.tile([P, NTILES, 2 * T], BF16, name="nbt")
        nc.scalar.dma_start(out=nbt[:], in_=nb.rearrange("(p i) t c -> p i (t c)", i=NTILES))
        w2t = keep.tile([P, 2, 2 * TU], U8, name="w2t", align_bytes=64)
        for q in range(4):
            nc.sync.dma_start(
                out=w2s[32 * q : 32 * q + 4, :, :].bitcast(I32),
                in_=w2_scales[:, 4 * q : 4 * q + 4, :].rearrange("g q n -> q g n").bitcast(I32),
            )
        for g in range(2):
            nc.sync.dma_start(out=w2t[:, g, :].bitcast(I32), in_=w2_words[g].bitcast(I32))
        for i in range(3, NTILES):
            load_x(i)

        ident = keep.tile([P, P], F32, name="ident")
        make_identity(nc, ident[:])


        w1p = keep.tile([P, 2, 2, 4, 2 * P], U8, name="w1p", align_bytes=64)
        w1sp = keep.tile([P, 2, 2, 4, P], U8, name="w1sp", align_bytes=64)
        b2f = keep.tile([P, P], F32, name="b2f")
        b2t = keep.tile([P, 2 * T], F32, name="b2t")
        flow = keep.tile([P, NTILES, 2 * T], F32, name="flow")

        def permute(q):
            for g in range(2):
                nc.vector.tensor_copy(
                    out=w1p[:, g, q, :, :].rearrange("p t (m b) -> p t m b", b=2),
                    in_=w1t[:, g, 1024 * q : 1024 * (q + 1)].rearrange("p (m t b) -> p t m b", t=4, b=2),
                )
            engine = nc.vector if q == 0 else nc.gpsimd
            engine.tensor_copy(
                out=w1sp[:, :, q, :, :],
                in_=w1s[:, :, 512 * q : 512 * (q + 1)].rearrange("p g (m t) -> p g t m", t=4),
            )

        def biases():
            nc.gpsimd.tensor_copy(out=b2f[:], in_=b2rows[:])
            nc.gpsimd.tensor_scalar(out=flow[:], in0=nbt[:], scalar1=16.0, scalar2=0.0, op0=ALU.mult, op1=ALU.add)
            b2ps = psum.tile([P, 512], F32, name="b2ps", tag="bank", bufs=8)
            nc.tensor.transpose(b2ps[:, 0:P], b2f[:], ident[:])
            nc.scalar.copy(out=b2t[:], in_=b2ps[:, 0 : 2 * T])


        state = {}

        def widen(i):
            xw = work.tile([P, D], BF16, name="xw%d" % i, tag="xw", bufs=3, align_bytes=64)
            for k in range(8):
                block = slice(P * k, P * (k + 1))
                if k < WIDEN_ON_VECTOR.get(i, 0):
                    nc.vector.tensor_scalar(
                        out=xw[:, block],
                        in0=xb[i][:, block].bitcast(FP8),
                        scalar1=xsc[:, i, k : k + 1],
                        scalar2=None,
                        op0=ALU.mult,
                    )
                else:
                    nc.scalar.activation(
                        out=xw[:, block], in_=xb[i][:, block].bitcast(FP8), func=ACT.Copy, scale=xsc[:, i, k : k + 1]
                    )
            state["xw", i] = xw

        def turn(i):
            words = state["xw", i][:].bitcast(F32)
            xt = psum.tile([P, 2, 2, P], F32, name="xt%d" % i, tag="bank", bufs=8)
            for g in range(2):
                for u in range(2):
                    nc.tensor.transpose(xt[:, g, u, :], words[:, 256 * g + u : 256 * (g + 1) : 2], ident[:])
            if i < 4:
                xg = work.tile([P, 2, P, 4], BF16, name="xg%d" % i, tag="xg", bufs=2, align_bytes=64)
                state["xg", i] = xg
                region = xg[:]
            else:
                if ("xgw", 1) not in state:
                    state["xgw", 1] = work.tile([P, 2, W, 4], BF16, name="xgw", tag="xgw", bufs=1, align_bytes=64)
                region = state["xgw", 1][:, :, P * (i - 4) : P * (i - 3), :]
            dst = region.rearrange("p g r e -> p g (r e)").bitcast(F32).rearrange("p g (r u) -> p g r u", u=2)
            src = xt[:].rearrange("p g u r -> p g r u")
            if i in TURN_ON_VECTOR:
                nc.vector.tensor_copy(out=dst, in_=src)
            else:
                nc.scalar.copy(out=dst, in_=src)

        def quant_x(i):
            xq = work.tile([P, 2 * P], U32, name="xq%d" % i, tag="xq", bufs=2, align_bytes=64)
            xs = work.tile([P, 2 * P], U8, name="xs%d" % i, tag="xs", bufs=2, align_bytes=64)
            nc.vector.quantize_mx(
                out=xq[:].bitcast(FP8X4), scales=xs[:], in_=state["xg", i][:].rearrange("p g n t -> p (g n t)")
            )
            hq = work.tile([P, 2 * P], U32, name="hq%d" % i, tag="hq", bufs=4, align_bytes=64)
            hs = work.tile([P, 2 * P], U8, name="hs%d" % i, tag="hs", bufs=4, align_bytes=64)
            state["x", i] = (xq, xs)
            state["h", i] = (hq, hs)

        def hidden(i, q):
            xq, xs = state["x", i]
            bank = psum.tile([P, 4, P], F32, name="h%d%d" % (i, q), tag="bank", bufs=8)
            for t in range(4):
                for g in range(2):
                    nc.tensor.matmul_mx(
                        out=bank[:, t, :],
                        lhsT=w1p[:, g, q, t, :].bitcast(FP4X4),
                        lhsT_scale=w1sp[:, g, q, t, :],
                        rhs=xq[:, g * P : (g + 1) * P].bitcast(FP8X4),
                        rhs_scale=xs[:, g * P : (g + 1) * P],
                        start=(g == 0),
                        stop=(g == 1),
                    )
            hr = work.tile([P, 4, P], BF16, name="hr%d%d" % (i, q), tag="hr", bufs=3, align_bytes=64)
            for t in range(4):
                if (i, q) in HIDDEN_ON_VECTOR:
                    nc.vector.tensor_scalar(
                        out=hr[:, t, :], in0=bank[:, t, :], scalar1=b1t[:, q, t : t + 1], scalar2=0.0, op0=ALU.add, op1=ALU.max
                    )
                else:
                    nc.scalar.activation(out=hr[:, t, :], in_=bank[:, t, :], func=ACT.Relu, bias=b1t[:, q, t : t + 1])
            state["hr", i, q] = hr

        def gather_h(i, q):
            hg = work.tile([P, P, 4], BF16, name="hg%d%d" % (i, q), tag="hg", bufs=3, align_bytes=64)
            src = state["hr", i, q][:].rearrange("p t n -> p n t")
            if (i, q) in GATHER_ON_SCALAR:
                nc.scalar.copy(out=hg[:], in_=src)
            else:
                nc.vector.tensor_copy(out=hg[:], in_=src)
            state["hg", i, q] = hg

        def quant_h(i, q):
            hq, hs = state["h", i]
            nc.vector.quantize_mx(
                out=hq[:, q * P : (q + 1) * P].bitcast(FP8X4),
                scales=hs[:, q * P : (q + 1) * P],
                in_=state["hg", i, q][:].rearrange("p n t -> p (n t)"),
            )

        def logits(i, b):
            hq, hs = state["h", i]
            if ("a", i) not in state:
                state["a", i] = work.tile([P, 2 * T, P], F32, name="a%d" % i, tag="a", bufs=3)
            a = state["a", i]
            bank = psum.tile([P, 4, P], F32, name="l%d_%d" % (i, b), tag="bank", bufs=8)
            blocks = range(4 * b, min(2 * T, 4 * b + 4))
            for r in blocks:
                for g in range(2):
                    nc.tensor.matmul_mx(
                        out=bank[:, r - 4 * b, :],
                        lhsT=w2t[:, g, 2 * P * r : 2 * P * (r + 1)].bitcast(FP4X4),
                        lhsT_scale=w2s[:, g, P * r : P * (r + 1)],
                        rhs=hq[:, g * P : (g + 1) * P].bitcast(FP8X4),
                        rhs_scale=hs[:, g * P : (g + 1) * P],
                        start=(g == 0),
                        stop=(g == 1),
                    )
            for r in blocks:
                if (i, b) in LOGITS_ON_VECTOR:
                    nc.vector.tensor_scalar(
                        out=a[:, r, :], in0=bank[:, r - 4 * b, :], scalar1=b2t[:, r : r + 1], scalar2=None, op0=ALU.add
                    )
                else:
                    nc.scalar.activation(out=a[:, r, :], in_=bank[:, r - 4 * b, :], func=ACT.Identity, bias=b2t[:, r : r + 1])

        def maximum(i, step):
            a = state["a", i]
            if step == 0:
                state["m", i] = work.tile([P, 8, P], F32, name="m%d" % i, tag="m", bufs=1)
                state["nm", i] = work.tile([P, 2, P], F32, name="nm%d" % i, tag="nm", bufs=3)
            m = state["m", i]
            if step == 0:
                nc.vector.tensor_tensor(out=m[:], in0=a[:, 0:8, :], in1=a[:, 8:16, :], op=ALU.max)
            elif step == 1:
                nc.vector.tensor_tensor(out=m[:, 0:4, :], in0=m[:, 0:4, :], in1=m[:, 4:8, :], op=ALU.max)
            elif step == 2:
                nc.vector.tensor_tensor(out=m[:, 0:2, :], in0=m[:, 0:2, :], in1=m[:, 2:4, :], op=ALU.max)
            elif step == 3:
                nc.vector.tensor_tensor(out=m[:, 0:2, :], in0=m[:, 0:2, :], in1=a[:, 16:18, :], op=ALU.max)
            else:
                if i in NEGATE_ON_SCALAR:
                    nc.scalar.activation(out=state["nm", i][:], in_=m[:, 0:2, :], func=ACT.Copy, scale=-1.0)
                else:
                    nc.vector.tensor_scalar(
                        out=state["nm", i][:], in0=m[:, 0:2, :], scalar1=-1.0, scalar2=None, op0=ALU.mult
                    )

        def quant_x_w(c, g):
            if ("xqw", c) not in state:
                state["xqw", c] = work.tile([P, 2, W], U32, name="xqw%d" % c, tag="xqw", bufs=1, align_bytes=64)
                state["xsw", c] = work.tile([P, 2, W], U8, name="xsw%d" % c, tag="xsw", bufs=1, align_bytes=64)
            nc.vector.quantize_mx(
                out=state["xqw", c][:, g, :].bitcast(FP8X4),
                scales=state["xsw", c][:, g, :],
                in_=state["xgw", c][:, g, :, :].rearrange("p n t -> p (n t)"),
            )

        def hidden_w(c, k):
            q, t = k // 4, k % 4
            xq, xs = state["xqw", c], state["xsw", c]
            if ("hrw", c, q) not in state:
                state["hrw", c, q] = work.tile([P, 4, W], BF16, name="hrw%d%d" % (c, q), tag="hrw", bufs=2, align_bytes=64)
            bank = psum.tile([P, W], F32, name="hw%d_%d" % (c, k), tag="bank", bufs=8)
            for g in range(2):
                nc.tensor.matmul_mx(
                    out=bank[:],
                    lhsT=w1p[:, g, q, t, :].bitcast(FP4X4),
                    lhsT_scale=w1sp[:, g, q, t, :],
                    rhs=xq[:, g, :].bitcast(FP8X4),
                    rhs_scale=xs[:, g, :],
                    start=(g == 0),
                    stop=(g == 1),
                )
            if (c, k) in WIDE_HIDDEN_ON_VECTOR:
                nc.vector.tensor_scalar(
                    out=state["hrw", c, q][:, t, :], in0=bank[:], scalar1=b1t[:, q, t : t + 1], scalar2=0.0, op0=ALU.add, op1=ALU.max
                )
            else:
                nc.scalar.activation(out=state["hrw", c, q][:, t, :], in_=bank[:], func=ACT.Relu, bias=b1t[:, q, t : t + 1])

        def gather_h_w(c, k):
            q, part = k // 2, k % 2
            if ("hgw", c, q) not in state:
                state["hgw", c, q] = work.tile([P, W, 4], BF16, name="hgw%d%d" % (c, q), tag="hgw", bufs=1, align_bytes=64)
            cols = slice(256 * part, 256 * (part + 1))
            dst, src = state["hgw", c, q][:, cols, :], state["hrw", c, q][:, :, cols].rearrange("p t n -> p n t")
            if (c, k) in WIDE_GATHER_ON_SCALAR:
                nc.scalar.copy(out=dst, in_=src)
            else:
                nc.vector.tensor_copy(out=dst, in_=src)

        def quant_h_w(c, q):
            if ("hqw", c) not in state:
                state["hqw", c] = work.tile([P, 2, W], U32, name="hqw%d" % c, tag="hqw", bufs=1, align_bytes=64)
                state["hsw", c] = work.tile([P, 2, W], U8, name="hsw%d" % c, tag="hsw", bufs=1, align_bytes=64)
            nc.vector.quantize_mx(
                out=state["hqw", c][:, q, :].bitcast(FP8X4),
                scales=state["hsw", c][:, q, :],
                in_=state["hgw", c, q][:].rearrange("p n t -> p (n t)"),
            )

        def logits_w(c, k):
            h, t = k // T, k % T
            hq, hs = state["hqw", c], state["hsw", c]
            if ("aw", c, h) not in state:
                state["aw", c, h] = work.tile([P, T, W], F32, name="aw%d%d" % (c, h), tag="aw%d" % h, bufs=1)
            col = U * t + P * h
            bank = psum.tile([P, W], F32, name="lw%d_%d" % (c, k), tag="bank", bufs=8)
            for g in range(2):
                nc.tensor.matmul_mx(
                    out=bank[:],
                    lhsT=w2t[:, g, 2 * col : 2 * (col + P)].bitcast(FP4X4),
                    lhsT_scale=w2s[:, g, col : col + P],
                    rhs=hq[:, g, :].bitcast(FP8X4),
                    rhs_scale=hs[:, g, :],
                    start=(g == 0),
                    stop=(g == 1),
                )
            bias = b2t[:, 2 * t + h : 2 * t + h + 1]
            if (c, k) in WIDE_LOGITS_ON_VECTOR:
                nc.vector.tensor_scalar(out=state["aw", c, h][:, t, :], in0=bank[:], scalar1=bias, scalar2=None, op0=ALU.add)
            else:
                nc.scalar.activation(out=state["aw", c, h][:, t, :], in_=bank[:], func=ACT.Identity, bias=bias)

        def maximum_w(c, k):
            h, step = k // 6, k % 6
            a = state["aw", c, h]
            if step == 0:
                state["mw", c, h] = work.tile([P, 2, W], F32, name="mw%d%d" % (c, h), tag="mw", bufs=1)
                if ("nmw", c) not in state:
                    state["nmw", c] = work.tile([P, 2, W], F32, name="nmw%d" % c, tag="nmw", bufs=1)
            m = state["mw", c, h]
            if step == 0:
                nc.vector.tensor_tensor(out=m[:], in0=a[:, 0:2, :], in1=a[:, 2:4, :], op=ALU.max)
            elif step < 3:
                nc.vector.tensor_tensor(out=m[:], in0=m[:], in1=a[:, 2 * step + 2 : 2 * step + 4, :], op=ALU.max)
            elif step == 3:
                nc.vector.tensor_tensor(out=m[:, 0, :], in0=m[:, 0, :], in1=m[:, 1, :], op=ALU.max)
            elif step == 4:
                nc.vector.tensor_tensor(out=m[:, 0, :], in0=m[:, 0, :], in1=a[:, 8, :], op=ALU.max)
            else:
                if (c, h) in WIDE_NEGATE_ON_SCALAR:
                    nc.scalar.activation(out=state["nmw", c][:, h, :], in_=m[:, 0, :], func=ACT.Copy, scale=-1.0)
                else:
                    nc.vector.tensor_scalar(
                        out=state["nmw", c][:, h, :], in0=m[:, 0, :], scalar1=-1.0, scalar2=None, op0=ALU.mult
                    )

        def weights(i, b):
            if i < 4:
                a = [state["a", i][:, h : 2 * T : 2, :] for h in range(2)]
                nm = state["nm", i]
                cols = slice(0, P)
            else:
                a = [state["aw", 1, h] for h in range(2)]
                nm = state["nmw", 1]
                cols = slice(P * (i - 4), P * (i - 3))
            if ("e", i) not in state:
                state["e", i] = work.tile([P, T, U], F32, name="e%d" % i, tag="e", bufs=3)
                state["acc", i] = work.tile([P, C, U], F32, name="acc%d" % i, tag="acc", bufs=5)
            e = state["e", i]
            taps = range(2 * b, min(T, 2 * b + 2))
            d = psum.tile([P, 2, U], F32, name="d%d_%d" % (i, b), tag="bank", bufs=8)
            for t in taps:
                for h in range(2):
                    dst = d[:, t - 2 * b, h * P : (h + 1) * P]
                    nc.tensor.matmul(dst, a[h][:, t, cols], ident[:], start=True, stop=False, is_transpose=True)
                    nc.tensor.matmul(dst, nm[:, h, cols], ident[:], start=False, stop=True, is_transpose=True)
            k = len(taps)
            nc.scalar.activation(out=e[:, 2 * b : 2 * b + k, :], in_=d[:, 0:k, :], func=ACT.Exp, scale=0.25)

        def first_product(i):
            for c in range(C):
                if (i, c) in SUMS_ON_TENSOR:
                    continue
                if i in FIRST_ON_VECTOR:
                    nc.vector.tensor_scalar(
                        out=state["acc", i][:, c, :], in0=state["e", i][:, 0, :], scalar1=flow[:, i, c : c + 1], scalar2=None, op0=ALU.mult
                    )
                else:
                    nc.scalar.activation(
                        out=state["acc", i][:, c, :], in_=state["e", i][:, 0, :], func=ACT.Copy, scale=flow[:, i, c : c + 1]
                    )

        def products(i, t):
            e, acc = state["e", i], state["acc", i]
            for c in range(C):
                if (i, c) not in SUMS_ON_TENSOR:
                    nc.vector.scalar_tensor_tensor(
                        out=acc[:, c, :],
                        in0=e[:, t, :],
                        scalar=flow[:, i, C * t + c : C * t + c + 1],
                        in1=acc[:, c, :],
                        op0=ALU.mult,
                        op1=ALU.add,
                    )

        def side_products(i, b):
            e = state["e", i]
            for c in range(C):
                if (i, c) in SUMS_ON_TENSOR:
                    if ("w", i, c) not in state:
                        state["w", i, c] = work.tile([P, T, U], F32, name="w%d%d" % (i, c), tag="a", bufs=3)
                    for t in range(2 * b, min(T, 2 * b + 2)):
                        factor = flow[:, i, C * t + c : C * t + c + 1]
                        dst = state["w", i, c][:, t, :]
                        if (i, b) in SIDE_ON_VECTOR:
                            nc.vector.tensor_scalar(out=dst, in0=e[:, t, :], scalar1=factor, scalar2=None, op0=ALU.mult)
                        else:
                            nc.scalar.activation(out=dst, in_=e[:, t, :], func=ACT.Copy, scale=factor)

        def side_sums(i):
            for c in range(C):
                if (i, c) in SUMS_ON_TENSOR:
                    bank = psum.tile([P, 512], F32, name="sum%d%d" % (i, c), tag="bank", bufs=8)
                    for h in range(2):
                        for t in range(T):
                            nc.tensor.matmul(
                                bank[:, h * P : (h + 1) * P],
                                state["w", i, c][:, t, h * P : (h + 1) * P],
                                ident[:],
                                start=(t == 0),
                                stop=(t == T - 1),
                                is_transpose=True,
                            )
                    sums = work.tile([P, 2, P], F32, name="sums%d%d" % (i, c), tag="sums", bufs=3)
                    nc.scalar.copy(out=sums[:].rearrange("p h n -> p (h n)"), in_=bank[:, 0:U])
                    state["sums", i, c] = sums

        def side_turn(i):
            for c in range(C):
                if (i, c) in SUMS_ON_TENSOR:
                    bank = psum.tile([P, 512], F32, name="back%d%d" % (i, c), tag="bank", bufs=8)
                    for h in range(2):
                        nc.tensor.transpose(bank[:, h * P : (h + 1) * P], state["sums", i, c][:, h, :], ident[:])
                    nc.scalar.copy(out=state["acc", i][:, c, :], in_=bank[:, 0:U])

        def denominator(i):
            e = state["e", i]
            n = GROUP_OF[i]
            if ("ds", n) not in state:
                state["ds", n] = work.tile([P, U * GROUPS[n]], F32, name="ds%d" % n, tag="ds", bufs=2)
            den = psum.tile([P, 2, P], F32, name="den%d" % i, tag="bank", bufs=8)
            for h in range(2):
                for t in range(T):
                    nc.tensor.matmul(
                        den[:, h, :], e[:, t, h * P : (h + 1) * P], ident[:], start=(t == 0), stop=(t == T - 1), is_transpose=True
                    )
            at = U * PLACE_OF[i]
            nc.scalar.copy(out=state["ds", n][:, at : at + U], in_=den[:].rearrange("p h n -> p (h n)"))

        def inverse(i, k):
            n = GROUP_OF[i]
            levels = 2 if GROUPS[n] == 1 else 3
            if PLACE_OF[i] != GROUPS[n] - 1 or k > 2 * levels:
                return
            if k == 0:
                state["tree", n] = [state["ds", n]]
            tree = state["tree", n]
            if k < levels:
                src = tree[k]
                half = src.shape[1] // 2
                dst = work.tile([P, half], F32, name="tree%d_%d" % (n, k), tag="tree%d" % half, bufs=2)
                nc.vector.tensor_tensor(out=dst[:], in0=src[:, 0:half], in1=src[:, half : 2 * half], op=ALU.mult)
                tree.append(dst)
            elif k == levels:
                dst = work.tile([P, 64], F32, name="inv%d" % n, tag="inv", bufs=3)
                nc.vector.reciprocal(out=dst[:], in_=tree[levels][:])
                state["inv", n] = dst
            else:
                src = tree[2 * levels - k]
                half = src.shape[1] // 2
                dst = work.tile([P, 2 * half], F32, name="inv%d_%d" % (n, k), tag="inv%d" % half, bufs=2)
                nc.vector.tensor_tensor(
                    out=dst[:].rearrange("p (a b) -> p a b", a=2),
                    in0=src[:].rearrange("p (a b) -> p a b", a=2)[:, ::-1, :],
                    in1=state["inv", n][:].unsqueeze(1).to_broadcast([P, 2, half]),
                    op=ALU.mult,
                )
                state["inv", n] = dst

        def turn_inverse(i):
            n = GROUP_OF[i]
            rd = psum.tile([P, 512], F32, name="rd%d" % i, tag="bank", bufs=8)
            for h in range(2):
                at = U * PLACE_OF[i] + P * h
                nc.tensor.transpose(rd[:, h * P : (h + 1) * P], state["inv", n][:, at : at + P], ident[:])
            state["rd", i] = rd

        def finish(i):
            o = work.tile([P, U, C], F32, name="o%d" % i, tag="o", bufs=3)
            nc.vector.tensor_tensor(
                out=o[:],
                in0=state["acc", i][:].rearrange("p c u -> p u c"),
                in1=state["rd", i][:, 0:U].unsqueeze(2).to_broadcast([P, U, C]),
                op=ALU.mult,
            )
            nc.sync.dma_start(out=out_view[:, i, :], in_=o[:].rearrange("p u c -> p (u c)"))

        def go(i, step, *args):
            if 0 <= i < NTILES:
                step(i, *args)

        with tc.manual_schedule():
            permute(0)
            permute(1)
            widen(0)
            widen(1)
            turn(0)
            quant_x(0)
            widen(2)
            turn(1)
            quant_x(1)
            hidden(0, 1)
            widen(3)
            hidden(0, 0)
            turn(2)
            widen(4)
            quant_x(2)
            gather_h(0, 1)
            quant_h(0, 1)
            widen(7)
            hidden(1, 1)
            hidden(1, 0)
            turn(3)
            widen(6)
            gather_h(0, 0)
            quant_x(3)
            gather_h(1, 1)
            turn(4)
            quant_h(1, 1)
            widen(5)
            quant_h(0, 0)
            hidden(2, 1)
            hidden(2, 0)
            gather_h(1, 0)
            turn(7)
            gather_h(2, 1)
            turn(6)
            biases()
            turn(5)
            quant_h(2, 1)
            quant_h(1, 0)
            hidden(3, 1)
            hidden(3, 0)
            gather_h(2, 0)
            gather_h(3, 1)
            quant_x_w(1, 0)
            quant_h(3, 1)
            quant_x_w(1, 1)
            quant_h(2, 0)
            gather_h(3, 0)
            quant_h(3, 0)
            logits(0, 0)
            logits(0, 3)
            logits(0, 1)
            logits(0, 2)
            logits(0, 4)
            hidden_w(1, 0)
            maximum(0, 0)
            maximum(0, 1)
            hidden_w(1, 3)
            hidden_w(1, 1)
            maximum(0, 2)
            logits(1, 0)
            maximum(0, 3)
            hidden_w(1, 2)
            logits(1, 3)
            logits(1, 1)
            logits(1, 2)
            gather_h_w(1, 0)
            hidden_w(1, 4)
            hidden_w(1, 7)
            maximum(0, 4)
            hidden_w(1, 6)
            gather_h_w(1, 1)
            hidden_w(1, 5)
            logits(1, 4)
            quant_h_w(1, 0)
            maximum(1, 0)
            maximum(1, 1)
            maximum(1, 2)
            logits(2, 0)
            gather_h_w(1, 2)
            maximum(1, 3)
            logits(2, 3)
            logits(2, 1)
            logits(2, 2)
            maximum(1, 4)
            logits(2, 4)
            weights(0, 0)
            first_product(0)
            weights(0, 3)
            gather_h_w(1, 3)
            weights(0, 4)
            maximum(2, 0)
            quant_h_w(1, 1)
            weights(0, 2)
            maximum(2, 1)
            weights(0, 1)
            maximum(2, 2)
            logits(3, 0)
            maximum(2, 3)
            logits(3, 3)
            logits(3, 1)
            products(0, 1)
            logits(3, 2)
            logits_w(1, 0)
            maximum(2, 4)
            logits_w(1, 3)
            products(0, 8)
            logits_w(1, 2)
            logits_w(1, 1)
            logits_w(1, 5)
            logits_w(1, 4)
            logits(3, 4)
            products(0, 6)
            logits_w(1, 7)
            logits_w(1, 6)
            weights(1, 0)
            first_product(1)
            products(0, 7)
            weights(1, 3)
            weights(1, 4)
            logits_w(1, 8)
            maximum(3, 0)
            logits_w(1, 9)
            logits_w(1, 10)
            logits_w(1, 11)
            logits_w(1, 12)
            logits_w(1, 14)
            logits_w(1, 16)
            logits_w(1, 13)
            products(0, 5)
            logits_w(1, 15)
            weights(1, 2)
            maximum(3, 1)
            maximum_w(1, 0)
            denominator(0)
            weights(1, 1)
            maximum(3, 2)
            maximum_w(1, 1)
            maximum(3, 3)
            maximum_w(1, 2)
            products(1, 1)
            products(0, 2)
            maximum_w(1, 3)
            maximum(3, 4)
            products(1, 8)
            maximum_w(1, 4)
            products(1, 6)
            inverse(0, 0)
            weights(2, 0)
            maximum_w(1, 5)
            first_product(2)
            products(1, 7)
            maximum_w(1, 6)
            weights(2, 3)
            weights(2, 4)
            inverse(0, 1)
            products(0, 4)
            maximum_w(1, 7)
            products(1, 5)
            weights(2, 2)
            denominator(1)
            weights(2, 1)
            logits_w(1, 17)
            maximum_w(1, 8)
            inverse(0, 2)
            products(0, 3)
            maximum_w(1, 9)
            inverse(0, 3)
            products(2, 1)
            products(1, 2)
            inverse(0, 4)
            products(2, 8)
            inverse(0, 5)
            products(2, 6)
            inverse(0, 6)
            inverse(1, 0)
            weights(3, 0)
            first_product(3)
            products(2, 7)
            weights(3, 3)
            weights(3, 4)
            inverse(1, 1)
            products(1, 4)
            maximum_w(1, 10)
            maximum_w(1, 11)
            products(2, 5)
            weights(3, 2)
            denominator(2)
            weights(3, 1)
            inverse(1, 2)
            products(1, 3)
            inverse(1, 3)
            products(3, 1)
            products(2, 2)
            inverse(1, 4)
            products(3, 8)
            inverse(1, 5)
            products(3, 6)
            inverse(1, 6)
            inverse(2, 0)
            weights(4, 0)
            first_product(4)
            products(3, 7)
            weights(4, 3)
            weights(4, 4)
            inverse(2, 1)
            products(2, 4)
            products(3, 5)
            weights(4, 2)
            denominator(3)
            weights(4, 1)
            inverse(2, 2)
            products(2, 3)
            inverse(2, 3)
            products(4, 1)
            products(3, 2)
            inverse(2, 4)
            products(4, 8)
            turn_inverse(0)
            finish(0)
            inverse(2, 5)
            products(4, 6)
            inverse(2, 6)
            inverse(3, 0)
            weights(5, 0)
            first_product(5)
            products(4, 7)
            weights(5, 3)
            weights(5, 4)
            inverse(3, 1)
            products(3, 4)
            products(4, 5)
            weights(5, 2)
            denominator(4)
            weights(5, 1)
            inverse(3, 2)
            products(3, 3)
            inverse(3, 3)
            products(5, 1)
            products(4, 2)
            inverse(3, 4)
            side_products(5, 2)
            products(5, 8)
            turn_inverse(1)
            finish(1)
            side_products(5, 0)
            inverse(3, 5)
            products(5, 6)
            inverse(3, 6)
            inverse(4, 0)
            weights(6, 0)
            first_product(6)
            products(5, 7)
            weights(6, 3)
            weights(6, 4)
            inverse(4, 1)
            products(4, 4)
            side_products(5, 1)
            products(5, 5)
            weights(6, 2)
            denominator(5)
            weights(6, 1)
            inverse(4, 2)
            products(4, 3)
            side_products(5, 3)
            side_products(5, 4)
            inverse(4, 3)
            products(6, 1)
            products(5, 2)
            inverse(4, 4)
            side_products(6, 2)
            products(6, 8)
            turn_inverse(2)
            finish(2)
            side_products(6, 0)
            inverse(4, 5)
            products(6, 6)
            inverse(4, 6)
            inverse(5, 0)
            weights(7, 0)
            first_product(7)
            products(6, 7)
            weights(7, 3)
            weights(7, 4)
            inverse(5, 1)
            products(5, 4)
            side_products(6, 1)
            products(6, 5)
            weights(7, 2)
            denominator(6)
            weights(7, 1)
            inverse(5, 2)
            products(5, 3)
            side_products(6, 3)
            side_products(6, 4)
            inverse(5, 3)
            products(7, 1)
            products(6, 2)
            inverse(5, 4)
            side_products(7, 2)
            products(7, 8)
            turn_inverse(3)
            finish(3)
            side_products(7, 0)
            inverse(5, 5)
            products(7, 6)
            inverse(5, 6)
            inverse(6, 0)
            products(7, 7)
            inverse(6, 1)
            products(6, 4)
            side_sums(5)
            side_products(7, 1)
            products(7, 5)
            denominator(7)
            inverse(6, 2)
            products(6, 3)
            side_products(7, 3)
            side_products(7, 4)
            inverse(6, 3)
            products(7, 2)
            inverse(6, 4)
            turn_inverse(4)
            finish(4)
            inverse(6, 5)
            inverse(6, 6)
            inverse(7, 0)
            inverse(7, 1)
            products(7, 4)
            side_sums(6)
            side_turn(5)
            inverse(7, 2)
            products(7, 3)
            inverse(7, 3)
            inverse(7, 4)
            turn_inverse(5)
            finish(5)
            inverse(7, 5)
            inverse(7, 6)
            side_sums(7)
            side_turn(6)
            turn_inverse(6)
            finish(6)
            side_turn(7)
            turn_inverse(7)
            finish(7)
